import numpy as np
import ml_dtypes


def mxq(x, axis, fmt="e4m3"):
    dtype, down = {"e4m3": (ml_dtypes.float8_e4m3fn, 7), "e5m2": (ml_dtypes.float8_e5m2, 14)}[fmt]
    v = np.moveaxis(np.asarray(x, np.float32).astype(ml_dtypes.bfloat16).astype(np.float64), axis, -1)
    blocks = v.reshape(v.shape[:-1] + (-1, 32))
    amax = np.abs(blocks).max(-1, keepdims=True)
    byte = np.maximum(np.where(amax > 0, np.frexp(amax)[1] - 1 + 127, 0) - down, 1)
    scale = np.exp2(byte - 127.0)
    codes = (blocks / scale).astype(np.float32).astype(dtype).astype(np.float64)
    return np.moveaxis((codes * scale).reshape(v.shape), -1, axis)


WIDE = False


def mx_kscale(k):
    if not WIDE:
        return np.ones(k)
    levels = np.array([10, -10, 5, -5, 0])
    if k % 512:
        return np.exp2(np.random.permutation(np.resize(levels, k // 32))).repeat(32)
    a = np.empty((k // 512, 16))
    for p in range(k // 512):
        a[p, :8] = np.random.permutation(np.resize(levels, 8))
        for g in range(8):
            far = levels[np.abs(levels - a[p, g]) >= 10]
            a[p, g + 8] = far[np.random.randint(len(far))]
    return np.exp2(a.ravel()).repeat(32)


def f64(x):
    return np.asarray(x).astype(np.float64)


def striped(idx):
    return np.tile(idx.reshape(-1, 16).T, (8, 1)).astype(np.uint16)


def unstriped(offs):
    return offs[:16].T.reshape(-1).astype(np.int64)


def pack_weight(w):
    k, n = w.shape
    w = f64(np.asarray(w, np.float32).astype(ml_dtypes.bfloat16)).reshape(k // 32, 32, n)
    amax = np.abs(w).max(1)
    byte = np.clip(np.where(amax > 0, np.frexp(amax)[1] - 1 + 127 - 7, 1), 1, 254)
    scaled = (w * np.exp2(127.0 - byte)[:, None, :]).reshape(k, n).astype(np.float32)
    words = np.ascontiguousarray(scaled.reshape(k // 512, 128, 4, n).transpose(0, 1, 3, 2)).astype(ml_dtypes.float8_e4m3fn).view(np.uint8)
    return words, np.ascontiguousarray(byte.astype(np.uint8).reshape(k // 512, 16, n))


def unpack_weight(words, scales):
    g, p, n, _ = words.shape
    vals = np.ascontiguousarray(words).view(ml_dtypes.float8_e4m3fn).astype(np.float64) * np.repeat(np.exp2(scales.astype(np.float64) - 127.0), 8, axis=1)[..., None]
    return vals.transpose(0, 1, 3, 2).reshape(g * 512, n)


K, T, S, V, N = 1024, 2048, 512, 256, 128


def setup_inputs():
    n = np.random.standard_normal
    s = mx_kscale(K)[:, None]
    packed_xT = pack_weight(n((K, T)) * s)
    return {
        "x_words": packed_xT[0],
        "x_scales": packed_xT[1],
        "w1": (n((K, N)) / np.sqrt(K) / s).astype(np.float32),
        "rate": (np.random.uniform(0.1, 0.6, (N, 1))).astype(np.float32),
        "offs": striped(np.random.permutation(T)[:S]),
        "cen": striped(np.random.permutation(S)[:V]),
        "pos1": striped(np.random.permutation(S)[:V]),
        "pos2": striped(np.random.permutation(S)[:V]),
    }


def reference(x_words, x_scales, w1, rate, offs, cen, pos1, pos2):
    xq = unpack_weight(x_words, x_scales)[:, unstriped(offs)]
    h = mxq(f64(w1), 0, "e4m3").T @ xq
    hc = h[:, unstriped(cen)]
    d0 = h[:, unstriped(pos1)] - hc
    d1 = h[:, unstriped(pos2)] - hc
    ss = d0 / (np.sqrt((d0) ** 2 + 1.0)) + d1 / (np.sqrt((d1) ** 2 + 1.0))
    return hc + f64(rate) * ss

@@ -1,0 +1,143 @@
+from contextlib import ExitStack
+
+import concourse.mybir as mybir
+
+K, T, S, V, N = 1024, 2048, 512, 256, 128
+FLOPS = 2 * K * N * S
+
+F32 = mybir.dt.float32
+BF16 = mybir.dt.bfloat16
+I32 = mybir.dt.int32
+U32 = mybir.dt.uint32
+U16 = mybir.dt.uint16
+U8 = mybir.dt.uint8
+FP8X4 = mybir.dt.float8_e4m3fn_x4
+ACT = mybir.ActivationFunctionType
+ALU = mybir.AluOpType
+
+P = 128
+PACK = 4
+PASSES = K // (P * PACK)
+HALF = S // 2
+VH = V // 2
+
+
+def tile_picked_ypm_tv_p_kernel(tc, x_words, x_scales, w1, rate, offs, cen, pos1, pos2, out):
+    nc = tc.nc
+    with ExitStack() as ctx:
+        keep = ctx.enter_context(tc.tile_pool(name="keep", bufs=1))
+        psum = ctx.enter_context(tc.psum_pool(name="psum", bufs=1))
+
+        offs_sb = keep.tile([P, S // 16], U16, name="offs_sb")
+        cen_sb = keep.tile([P, V // 16], U16, name="cen_sb")
+        pos_sb = [keep.tile([P, V // 16], U16, name=f"pos_sb{i}") for i in range(2)]
+        scale_table = keep.tile([P, T], U8, name="scale_table", align_bytes=64)
+        word_table = [keep.tile([P, T], U32, name=f"word_table{g}", align_bytes=64) for g in range(PASSES)]
+        w_raw = keep.tile([P, PASSES, PACK, N], F32, name="w_raw")
+        rate_sb = keep.tile([P, 1], F32, name="rate_sb")
+        ones = keep.tile([P, 1], F32, name="ones")
+        unit = keep.tile([P, 1], F32, name="unit")
+
+        nc.vector.memset(scale_table[:].bitcast(I32), 0)
+        nc.vector.memset(ones[:], 1.0)
+
+        nc.sync.dma_start(out=w_raw[:], in_=w1.rearrange("(g p j) m -> p g j m", g=PASSES, j=PACK))
+        nc.sync.dma_start(offs_sb[:], offs)
+        for g in range(PASSES):
+            nc.sync.dma_start(
+                out=word_table[g][:].bitcast(I32),
+                in_=x_words[g].rearrange("p n t -> p (n t)").bitcast(I32),
+            )
+        nc.sync.dma_start(cen_sb[:], cen)
+        nc.sync.dma_start(pos_sb[0][:], pos1)
+        nc.sync.dma_start(pos_sb[1][:], pos2)
+        for q in range(4):
+            queue = nc.scalar if q < 2 else nc.gpsimd
+            queue.dma_start(
+                out=scale_table[32 * q : 32 * q + 4 * PASSES, :].bitcast(I32),
+                in_=x_scales[:, 4 * q : 4 * q + 4, :].bitcast(I32),
+            )
+        nc.sync.dma_start(out=rate_sb[:], in_=rate)
+
+        nc.scalar.activation(unit[:], ones[:], ACT.Abs_reciprocal_sqrt)
+
+        w_bf = keep.tile([P, PASSES, N, PACK], BF16, name="w_bf", align_bytes=64)
+        for g in range(PASSES):
+            nc.scalar.copy(out=w_bf[:, g], in_=w_raw[:, g].rearrange("p j m -> p m j"))
+        w_codes = keep.tile([P, PASSES * N], U32, name="w_codes", align_bytes=64)
+        w_scales = keep.tile([P, PASSES * N], U8, name="w_scales", align_bytes=64)
+        nc.vector.quantize_mx(
+            out=w_codes[:].bitcast(FP8X4),
+            scales=w_scales[:],
+            in_=w_bf[:].rearrange("p g m j -> p (g m j)"),
+        )
+
+        x_sc = keep.tile([P, S], U8, name="x_sc", align_bytes=64)
+        nc.vector.tensor_copy(x_sc[:], scale_table[:].indirect(offs_sb[:]))
+
+        h = keep.tile([P, S], F32, name="h", align_bytes=64)
+        acc = [psum.tile([P, HALF], F32, name=f"acc{a}") for a in range(2)]
+        for g in range(PASSES):
+            for a in range(2):
+                cols = slice(a * HALF, (a + 1) * HALF)
+                x_codes = keep.tile([P, HALF], U32, name=f"x_codes{g}{a}", align_bytes=64)
+                nc.vector.tensor_copy(
+                    x_codes[:], word_table[g][:].indirect(offs_sb[:, a * HALF // 16 : (a + 1) * HALF // 16])
+                )
+                nc.tensor.matmul_mx(
+                    out=acc[a][:],
+                    lhsT=w_codes[:, g * N : (g + 1) * N].bitcast(FP8X4),
+                    lhsT_scale=w_scales[:, g * N : (g + 1) * N],
+                    rhs=x_codes[:].bitcast(FP8X4),
+                    rhs_scale=x_sc[4 * g :, cols],
+                    start=(g == 0),
+                    stop=(g == PASSES - 1),
+                )
+        nc.scalar.copy(out=h[:, :HALF], in_=acc[0][:])
+        nc.vector.tensor_copy(out=h[:, HALF:], in_=acc[1][:])
+
+        halves = [slice(b * VH, (b + 1) * VH) for b in range(2)]
+        list_halves = [slice(b * VH // 16, (b + 1) * VH // 16) for b in range(2)]
+        hc = keep.tile([P, V], F32, name="hc")
+        d = [keep.tile([P, V], F32, name=f"d{i}") for i in range(2)]
+        sq = [keep.tile([P, V], F32, name=f"sq{i}") for i in range(2)]
+        r = [keep.tile([P, V], F32, name=f"r{i}") for i in range(2)]
+        t = [keep.tile([P, V], F32, name=f"t{i}") for i in range(2)]
+        u = keep.tile([P, V], F32, name="u")
+        res = keep.tile([P, V], F32, name="res")
+        for b in range(2):
+            nc.vector.tensor_copy(hc[:, halves[b]], h[:].indirect(cen_sb[:, list_halves[b]]))
+        for i in range(2):
+            for b in range(2):
+                nc.vector.tensor_tensor(
+                    d[i][:, halves[b]], h[:].indirect(pos_sb[i][:, list_halves[b]]), hc[:, halves[b]], ALU.subtract
+                )
+
+        def square(i, b):
+            nc.scalar.activation(sq[i][:, halves[b]], d[i][:, halves[b]], ACT.Square)
+
+        def damp(i, b):
+            nc.scalar.activation(r[i][:, halves[b]], sq[i][:, halves[b]], ACT.Abs_reciprocal_sqrt, bias=unit[:])
+
+        def pull(i, b):
+            nc.vector.scalar_tensor_tensor(
+                t[i][:, halves[b]], d[i][:, halves[b]], rate_sb[:], r[i][:, halves[b]], ALU.mult, ALU.mult
+            )
+
+        square(0, 0)
+        damp(0, 0)
+        square(0, 1)
+        damp(0, 1)
+        square(1, 0)
+        damp(1, 0)
+        square(1, 1)
+        damp(1, 1)
+        pull(0, 0)
+        pull(0, 1)
+        nc.vector.tensor_tensor(u[:, halves[0]], t[0][:, halves[0]], hc[:, halves[0]], ALU.add)
+        pull(1, 0)
+        nc.vector.tensor_tensor(u[:, halves[1]], t[0][:, halves[1]], hc[:, halves[1]], ALU.add)
+        pull(1, 1)
+        for b in range(2):
+            nc.vector.tensor_tensor(res[:, halves[b]], u[:, halves[b]], t[1][:, halves[b]], ALU.add)
+            nc.sync.dma_start(out=out[:, halves[b]], in_=res[:, halves[b]])

@@ -42,6 +42,11 @@ def tile_picked_ypm_tv_p_kernel(tc, x_words, x_scales, w1, rate, offs, cen, pos1
         nc.vector.memset(ones[:], 1.0)
 
         nc.sync.dma_start(out=w_raw[:], in_=w1.rearrange("(g p j) m -> p g j m", g=PASSES, j=PACK))
+        for q in range(4):
+            nc.sync.dma_start(
+                out=scale_table[32 * q : 32 * q + 4 * PASSES, :].bitcast(I32),
+                in_=x_scales[:, 4 * q : 4 * q + 4, :].bitcast(I32),
+            )
         nc.sync.dma_start(offs_sb[:], offs)
         for g in range(PASSES):
             nc.sync.dma_start(
@@ -51,12 +56,6 @@ def tile_picked_ypm_tv_p_kernel(tc, x_words, x_scales, w1, rate, offs, cen, pos1
         nc.sync.dma_start(cen_sb[:], cen)
         nc.sync.dma_start(pos_sb[0][:], pos1)
         nc.sync.dma_start(pos_sb[1][:], pos2)
-        for q in range(4):
-            queue = nc.scalar if q < 2 else nc.gpsimd
-            queue.dma_start(
-                out=scale_table[32 * q : 32 * q + 4 * PASSES, :].bitcast(I32),
-                in_=x_scales[:, 4 * q : 4 * q + 4, :].bitcast(I32),
-            )
         nc.sync.dma_start(out=rate_sb[:], in_=rate)
 
         nc.scalar.activation(unit[:], ones[:], ACT.Abs_reciprocal_sqrt)
@@ -76,28 +75,29 @@ def tile_picked_ypm_tv_p_kernel(tc, x_words, x_scales, w1, rate, offs, cen, pos1
         nc.vector.tensor_copy(x_sc[:], scale_table[:].indirect(offs_sb[:]))
 
         h = keep.tile([P, S], F32, name="h", align_bytes=64)
-        acc = [psum.tile([P, HALF], F32, name=f"acc{a}") for a in range(2)]
+        QUART = HALF // 2
+        spans = [[(0, HALF)], [(HALF, QUART), (HALF + QUART, QUART)]]
+        acc = {lo: psum.tile([P, n], F32, name=f"acc{lo}") for span in spans for lo, n in span}
         for g in range(PASSES):
             for a in range(2):
-                cols = slice(a * HALF, (a + 1) * HALF)
                 x_codes = keep.tile([P, HALF], U32, name=f"x_codes{g}{a}", align_bytes=64)
                 nc.vector.tensor_copy(
                     x_codes[:], word_table[g][:].indirect(offs_sb[:, a * HALF // 16 : (a + 1) * HALF // 16])
                 )
-                nc.tensor.matmul_mx(
-                    out=acc[a][:],
-                    lhsT=w_codes[:, g * N : (g + 1) * N].bitcast(FP8X4),
-                    lhsT_scale=w_scales[:, g * N : (g + 1) * N],
-                    rhs=x_codes[:].bitcast(FP8X4),
-                    rhs_scale=x_sc[4 * g :, cols],
-                    start=(g == 0),
-                    stop=(g == PASSES - 1),
-                )
+                for lo, n in spans[a]:
+                    nc.tensor.matmul_mx(
+                        out=acc[lo][:],
+                        lhsT=w_codes[:, g * N : (g + 1) * N].bitcast(FP8X4),
+                        lhsT_scale=w_scales[:, g * N : (g + 1) * N],
+                        rhs=x_codes[:, lo - a * HALF : lo - a * HALF + n].bitcast(FP8X4),
+                        rhs_scale=x_sc[4 * g :, lo : lo + n],
+                        start=(g == 0),
+                        stop=(g == PASSES - 1),
+                    )
         nc.scalar.copy(out=h[:, :HALF], in_=acc[0][:])
-        nc.vector.tensor_copy(out=h[:, HALF:], in_=acc[1][:])
+        nc.scalar.copy(out=h[:, HALF : HALF + QUART], in_=acc[HALF][:])
+        nc.vector.tensor_copy(out=h[:, HALF + QUART :], in_=acc[HALF + QUART][:])
 
-        halves = [slice(b * VH, (b + 1) * VH) for b in range(2)]
-        list_halves = [slice(b * VH // 16, (b + 1) * VH // 16) for b in range(2)]
         hc = keep.tile([P, V], F32, name="hc")
         d = [keep.tile([P, V], F32, name=f"d{i}") for i in range(2)]
         sq = [keep.tile([P, V], F32, name=f"sq{i}") for i in range(2)]
@@ -105,39 +105,25 @@ def tile_picked_ypm_tv_p_kernel(tc, x_words, x_scales, w1, rate, offs, cen, pos1
         t = [keep.tile([P, V], F32, name=f"t{i}") for i in range(2)]
         u = keep.tile([P, V], F32, name="u")
         res = keep.tile([P, V], F32, name="res")
-        for b in range(2):
-            nc.vector.tensor_copy(hc[:, halves[b]], h[:].indirect(cen_sb[:, list_halves[b]]))
+        chunks = [[(0, 128), (128, 256)], [(0, 128), (128, 192), (192, 256)]]
+        for lo, hi in [(0, 128), (128, 256)]:
+            nc.vector.tensor_copy(hc[:, lo:hi], h[:].indirect(cen_sb[:, lo // 16 : hi // 16]))
         for i in range(2):
-            for b in range(2):
+            for lo, hi in chunks[i]:
                 nc.vector.tensor_tensor(
-                    d[i][:, halves[b]], h[:].indirect(pos_sb[i][:, list_halves[b]]), hc[:, halves[b]], ALU.subtract
+                    d[i][:, lo:hi], h[:].indirect(pos_sb[i][:, lo // 16 : hi // 16]), hc[:, lo:hi], ALU.subtract
                 )
-
-        def square(i, b):
-            nc.scalar.activation(sq[i][:, halves[b]], d[i][:, halves[b]], ACT.Square)
-
-        def damp(i, b):
-            nc.scalar.activation(r[i][:, halves[b]], sq[i][:, halves[b]], ACT.Abs_reciprocal_sqrt, bias=unit[:])
-
-        def pull(i, b):
-            nc.vector.scalar_tensor_tensor(
-                t[i][:, halves[b]], d[i][:, halves[b]], rate_sb[:], r[i][:, halves[b]], ALU.mult, ALU.mult
-            )
-
-        square(0, 0)
-        damp(0, 0)
-        square(0, 1)
-        damp(0, 1)
-        square(1, 0)
-        damp(1, 0)
-        square(1, 1)
-        damp(1, 1)
-        pull(0, 0)
-        pull(0, 1)
-        nc.vector.tensor_tensor(u[:, halves[0]], t[0][:, halves[0]], hc[:, halves[0]], ALU.add)
-        pull(1, 0)
-        nc.vector.tensor_tensor(u[:, halves[1]], t[0][:, halves[1]], hc[:, halves[1]], ALU.add)
-        pull(1, 1)
-        for b in range(2):
-            nc.vector.tensor_tensor(res[:, halves[b]], u[:, halves[b]], t[1][:, halves[b]], ALU.add)
-            nc.sync.dma_start(out=out[:, halves[b]], in_=res[:, halves[b]])
+                nc.scalar.activation(sq[i][:, lo:hi], d[i][:, lo:hi], ACT.Square)
+                nc.scalar.activation(r[i][:, lo:hi], sq[i][:, lo:hi], ACT.Abs_reciprocal_sqrt, bias=unit[:])
+        for i in range(2):
+            for lo, hi in chunks[i]:
+                nc.vector.scalar_tensor_tensor(
+                    t[i][:, lo:hi], d[i][:, lo:hi], rate_sb[:], r[i][:, lo:hi], ALU.mult, ALU.mult
+                )
+            if i == 0:
+                for lo, hi in chunks[0]:
+                    nc.vector.tensor_tensor(u[:, lo:hi], t[0][:, lo:hi], hc[:, lo:hi], ALU.add)
+        for lo, hi in chunks[1]:
+            nc.vector.tensor_tensor(res[:, lo:hi], u[:, lo:hi], t[1][:, lo:hi], ALU.add)
+        for lo, hi in [(0, 128), (128, 256)]:
+            nc.sync.dma_start(out=out[:, lo:hi], in_=res[:, lo:hi])

@@ -31,22 +31,23 @@ def tile_picked_ypm_tv_p_kernel(tc, x_words, x_scales, w1, rate, offs, cen, pos1
         offs_sb = keep.tile([P, S // 16], U16, name="offs_sb")
         cen_sb = keep.tile([P, V // 16], U16, name="cen_sb")
         pos_sb = [keep.tile([P, V // 16], U16, name=f"pos_sb{i}") for i in range(2)]
-        scale_table = keep.tile([P, T], U8, name="scale_table", align_bytes=64)
+        scale_table = keep.tile([P, PASSES, T], U8, name="scale_table", tag="scale_table", align_bytes=64)
         word_table = [keep.tile([P, T], U32, name=f"word_table{g}", align_bytes=64) for g in range(PASSES)]
         w_raw = keep.tile([P, PASSES, PACK, N], F32, name="w_raw")
         rate_sb = keep.tile([P, 1], F32, name="rate_sb")
         ones = keep.tile([P, 1], F32, name="ones")
         unit = keep.tile([P, 1], F32, name="unit")
 
-        nc.vector.memset(scale_table[:].bitcast(I32), 0)
+        nc.vector.memset(scale_table[:].rearrange("p g t -> p (g t)").bitcast(I32), 0)
         nc.vector.memset(ones[:], 1.0)
+        x_sc = keep.tile([P, PASSES * S], U8, name="x_sc", align_bytes=64)
+        nc.vector.memset(x_sc[:].bitcast(I32), 0)
 
         nc.sync.dma_start(out=w_raw[:], in_=w1.rearrange("(g p j) m -> p g j m", g=PASSES, j=PACK))
-        for q in range(4):
-            nc.sync.dma_start(
-                out=scale_table[32 * q : 32 * q + 4 * PASSES, :].bitcast(I32),
-                in_=x_scales[:, 4 * q : 4 * q + 4, :].bitcast(I32),
-            )
+        nc.sync.dma_start(
+            out=scale_table[4:P:8].bitcast(I32),
+            in_=x_scales.rearrange("g b t -> b g t").bitcast(I32),
+        )
         nc.sync.dma_start(offs_sb[:], offs)
         for g in range(PASSES):
             nc.sync.dma_start(
@@ -56,14 +57,23 @@ def tile_picked_ypm_tv_p_kernel(tc, x_words, x_scales, w1, rate, offs, cen, pos1
         nc.sync.dma_start(cen_sb[:], cen)
         nc.sync.dma_start(pos_sb[0][:], pos1)
         nc.sync.dma_start(pos_sb[1][:], pos2)
-        nc.sync.dma_start(out=rate_sb[:], in_=rate)
+        nc.gpsimd.dma_start(out=rate_sb[:], in_=rate)
+
+        picked_sc = keep.tile([P, PASSES * S], U8, name="picked_sc", align_bytes=64)
+        for g in range(PASSES):
+            nc.vector.tensor_copy(picked_sc[:, g * S : (g + 1) * S], scale_table[:, g, :].indirect(offs_sb[:]))
+        for q in range(4):
+            nc.sync.dma_start(
+                out=x_sc[32 * q : 32 * q + 4, :].bitcast(I32),
+                in_=picked_sc[32 * q + 4 : 32 * q + 32 : 8, :].bitcast(I32),
+            )
 
         nc.scalar.activation(unit[:], ones[:], ACT.Abs_reciprocal_sqrt)
 
         w_bf = keep.tile([P, PASSES, N, PACK], BF16, name="w_bf", align_bytes=64)
         for g in range(PASSES):
             nc.scalar.copy(out=w_bf[:, g], in_=w_raw[:, g].rearrange("p j m -> p m j"))
-        w_codes = keep.tile([P, PASSES * N], U32, name="w_codes", align_bytes=64)
+        w_codes = keep.tile([P, PASSES * N], U32, name="w_codes", tag="scale_table", align_bytes=64)
         w_scales = keep.tile([P, PASSES * N], U8, name="w_scales", align_bytes=64)
         nc.vector.quantize_mx(
             out=w_codes[:].bitcast(FP8X4),
@@ -71,8 +81,6 @@ def tile_picked_ypm_tv_p_kernel(tc, x_words, x_scales, w1, rate, offs, cen, pos1
             in_=w_bf[:].rearrange("p g m j -> p (g m j)"),
         )
 
-        x_sc = keep.tile([P, S], U8, name="x_sc", align_bytes=64)
-        nc.vector.tensor_copy(x_sc[:], scale_table[:].indirect(offs_sb[:]))
 
         h = keep.tile([P, S], F32, name="h", align_bytes=64)
         QUART = HALF // 2
@@ -90,7 +98,7 @@ def tile_picked_ypm_tv_p_kernel(tc, x_words, x_scales, w1, rate, offs, cen, pos1
                         lhsT=w_codes[:, g * N : (g + 1) * N].bitcast(FP8X4),
                         lhsT_scale=w_scales[:, g * N : (g + 1) * N],
                         rhs=x_codes[:, lo - a * HALF : lo - a * HALF + n].bitcast(FP8X4),
-                        rhs_scale=x_sc[4 * g :, lo : lo + n],
+                        rhs_scale=x_sc[:, g * S + lo : g * S + lo + n],
                         start=(g == 0),
                         stop=(g == PASSES - 1),
                     )

@@ -31,21 +31,19 @@ def tile_picked_ypm_tv_p_kernel(tc, x_words, x_scales, w1, rate, offs, cen, pos1
         offs_sb = keep.tile([P, S // 16], U16, name="offs_sb")
         cen_sb = keep.tile([P, V // 16], U16, name="cen_sb")
         pos_sb = [keep.tile([P, V // 16], U16, name=f"pos_sb{i}") for i in range(2)]
-        scale_table = keep.tile([P, PASSES, T], U8, name="scale_table", tag="scale_table", align_bytes=64)
+        scale_table = keep.tile([P, T], U8, name="scale_table", align_bytes=64)
         word_table = [keep.tile([P, T], U32, name=f"word_table{g}", align_bytes=64) for g in range(PASSES)]
         w_raw = keep.tile([P, PASSES, PACK, N], F32, name="w_raw")
-        rate_sb = keep.tile([P, 1], F32, name="rate_sb")
         ones = keep.tile([P, 1], F32, name="ones")
         unit = keep.tile([P, 1], F32, name="unit")
 
-        nc.vector.memset(scale_table[:].rearrange("p g t -> p (g t)").bitcast(I32), 0)
+        nc.vector.memset(scale_table[:].bitcast(I32), 0)
         nc.vector.memset(ones[:], 1.0)
-        x_sc = keep.tile([P, PASSES * S], U8, name="x_sc", align_bytes=64)
-        nc.vector.memset(x_sc[:].bitcast(I32), 0)
+        x_sc = keep.tile([P, S], U8, name="x_sc", align_bytes=64)
 
         nc.sync.dma_start(out=w_raw[:], in_=w1.rearrange("(g p j) m -> p g j m", g=PASSES, j=PACK))
         nc.sync.dma_start(
-            out=scale_table[4:P:8].bitcast(I32),
+            out=scale_table[0:96:3].bitcast(I32),
             in_=x_scales.rearrange("g b t -> b g t").bitcast(I32),
         )
         nc.sync.dma_start(offs_sb[:], offs)
@@ -57,23 +55,24 @@ def tile_picked_ypm_tv_p_kernel(tc, x_words, x_scales, w1, rate, offs, cen, pos1
         nc.sync.dma_start(cen_sb[:], cen)
         nc.sync.dma_start(pos_sb[0][:], pos1)
         nc.sync.dma_start(pos_sb[1][:], pos2)
-        nc.gpsimd.dma_start(out=rate_sb[:], in_=rate)
 
-        picked_sc = keep.tile([P, PASSES * S], U8, name="picked_sc", align_bytes=64)
-        for g in range(PASSES):
-            nc.vector.tensor_copy(picked_sc[:, g * S : (g + 1) * S], scale_table[:, g, :].indirect(offs_sb[:]))
-        for q in range(4):
+        picked_sc = keep.tile([P, S], U8, name="picked_sc", tag="picked_sc", align_bytes=64)
+        nc.vector.tensor_copy(picked_sc[:], scale_table[:].indirect(offs_sb[:]))
+        for j in range(4):
             nc.sync.dma_start(
-                out=x_sc[32 * q : 32 * q + 4, :].bitcast(I32),
-                in_=picked_sc[32 * q + 4 : 32 * q + 32 : 8, :].bitcast(I32),
+                out=x_sc[j:P:4, :].bitcast(I32),
+                in_=picked_sc[6 * j : 6 * j + 96 : 3, :].bitcast(I32),
             )
+
+        rate_sb = keep.tile([P, 1], F32, name="rate_sb", tag="picked_sc", align_bytes=64)
+        nc.sync.dma_start(out=rate_sb[:], in_=rate)
 
         nc.scalar.activation(unit[:], ones[:], ACT.Abs_reciprocal_sqrt)
 
         w_bf = keep.tile([P, PASSES, N, PACK], BF16, name="w_bf", align_bytes=64)
         for g in range(PASSES):
             nc.scalar.copy(out=w_bf[:, g], in_=w_raw[:, g].rearrange("p j m -> p m j"))
-        w_codes = keep.tile([P, PASSES * N], U32, name="w_codes", tag="scale_table", align_bytes=64)
+        w_codes = keep.tile([P, PASSES * N], U32, name="w_codes", align_bytes=64)
         w_scales = keep.tile([P, PASSES * N], U8, name="w_scales", align_bytes=64)
         nc.vector.quantize_mx(
             out=w_codes[:].bitcast(FP8X4),
@@ -98,7 +97,7 @@ def tile_picked_ypm_tv_p_kernel(tc, x_words, x_scales, w1, rate, offs, cen, pos1
                         lhsT=w_codes[:, g * N : (g + 1) * N].bitcast(FP8X4),
                         lhsT_scale=w_scales[:, g * N : (g + 1) * N],
                         rhs=x_codes[:, lo - a * HALF : lo - a * HALF + n].bitcast(FP8X4),
-                        rhs_scale=x_sc[:, g * S + lo : g * S + lo + n],
+                        rhs_scale=x_sc[4 * g :, lo : lo + n],
                         start=(g == 0),
                         stop=(g == PASSES - 1),
                     )

@@ -59,7 +59,7 @@ def tile_picked_ypm_tv_p_kernel(tc, x_words, x_scales, w1, rate, offs, cen, pos1
         picked_sc = keep.tile([P, S], U8, name="picked_sc", tag="picked_sc", align_bytes=64)
         nc.vector.tensor_copy(picked_sc[:], scale_table[:].indirect(offs_sb[:]))
         for j in range(4):
-            nc.sync.dma_start(
+            nc.scalar.dma_start(
                 out=x_sc[j:P:4, :].bitcast(I32),
                 in_=picked_sc[6 * j : 6 * j + 96 : 3, :].bitcast(I32),
             )

@@ -102,8 +102,8 @@ def tile_picked_ypm_tv_p_kernel(tc, x_words, x_scales, w1, rate, offs, cen, pos1
                         stop=(g == PASSES - 1),
                     )
         nc.scalar.copy(out=h[:, :HALF], in_=acc[0][:])
-        nc.scalar.copy(out=h[:, HALF : HALF + QUART], in_=acc[HALF][:])
-        nc.vector.tensor_copy(out=h[:, HALF + QUART :], in_=acc[HALF + QUART][:])
+        nc.vector.tensor_copy(out=h[:, HALF : HALF + QUART], in_=acc[HALF][:])
+        nc.scalar.copy(out=h[:, HALF + QUART :], in_=acc[HALF + QUART][:])
 
         hc = keep.tile([P, V], F32, name="hc")
         d = [keep.tile([P, V], F32, name=f"d{i}") for i in range(2)]
@@ -112,25 +112,26 @@ def tile_picked_ypm_tv_p_kernel(tc, x_words, x_scales, w1, rate, offs, cen, pos1
         t = [keep.tile([P, V], F32, name=f"t{i}") for i in range(2)]
         u = keep.tile([P, V], F32, name="u")
         res = keep.tile([P, V], F32, name="res")
-        chunks = [[(0, 128), (128, 256)], [(0, 128), (128, 192), (192, 256)]]
-        for lo, hi in [(0, 128), (128, 256)]:
-            nc.vector.tensor_copy(hc[:, lo:hi], h[:].indirect(cen_sb[:, lo // 16 : hi // 16]))
+        halves = [slice(0, VH), slice(VH, V)]
+        lists = [slice(0, VH // 16), slice(VH // 16, V // 16)]
+        for c, o in zip(halves, lists):
+            nc.vector.tensor_copy(hc[:, c], h[:].indirect(cen_sb[:, o]))
         for i in range(2):
-            for lo, hi in chunks[i]:
-                nc.vector.tensor_tensor(
-                    d[i][:, lo:hi], h[:].indirect(pos_sb[i][:, lo // 16 : hi // 16]), hc[:, lo:hi], ALU.subtract
-                )
-                nc.scalar.activation(sq[i][:, lo:hi], d[i][:, lo:hi], ACT.Square)
-                nc.scalar.activation(r[i][:, lo:hi], sq[i][:, lo:hi], ACT.Abs_reciprocal_sqrt, bias=unit[:])
-        for i in range(2):
-            for lo, hi in chunks[i]:
-                nc.vector.scalar_tensor_tensor(
-                    t[i][:, lo:hi], d[i][:, lo:hi], rate_sb[:], r[i][:, lo:hi], ALU.mult, ALU.mult
-                )
-            if i == 0:
-                for lo, hi in chunks[0]:
-                    nc.vector.tensor_tensor(u[:, lo:hi], t[0][:, lo:hi], hc[:, lo:hi], ALU.add)
-        for lo, hi in chunks[1]:
-            nc.vector.tensor_tensor(res[:, lo:hi], u[:, lo:hi], t[1][:, lo:hi], ALU.add)
-        for lo, hi in [(0, 128), (128, 256)]:
-            nc.sync.dma_start(out=out[:, lo:hi], in_=res[:, lo:hi])
+            for c, o in zip(halves, lists):
+                nc.vector.tensor_tensor(d[i][:, c], h[:].indirect(pos_sb[i][:, o]), hc[:, c], ALU.subtract)
+        steps = [(i, c) for i in range(2) for c in halves]
+        for k in range(len(steps) + 1):
+            if k < len(steps):
+                i, c = steps[k]
+                nc.scalar.activation(sq[i][:, c], d[i][:, c], ACT.Square)
+            if k > 0:
+                i, c = steps[k - 1]
+                nc.scalar.activation(r[i][:, c], sq[i][:, c], ACT.Abs_reciprocal_sqrt, bias=unit[:])
+        for c in halves:
+            nc.vector.scalar_tensor_tensor(t[0][:, c], d[0][:, c], rate_sb[:], r[0][:, c], ALU.mult, ALU.mult)
+        for c in halves:
+            nc.vector.tensor_tensor(u[:, c], t[0][:, c], hc[:, c], ALU.add)
+            nc.vector.scalar_tensor_tensor(t[1][:, c], d[1][:, c], rate_sb[:], r[1][:, c], ALU.mult, ALU.mult)
+        for c in halves:
+            nc.vector.tensor_tensor(res[:, c], u[:, c], t[1][:, c], ALU.add)
+            nc.sync.dma_start(out=out[:, c], in_=res[:, c])

@@ -112,26 +112,49 @@ def tile_picked_ypm_tv_p_kernel(tc, x_words, x_scales, w1, rate, offs, cen, pos1
         t = [keep.tile([P, V], F32, name=f"t{i}") for i in range(2)]
         u = keep.tile([P, V], F32, name="u")
         res = keep.tile([P, V], F32, name="res")
-        halves = [slice(0, VH), slice(VH, V)]
-        lists = [slice(0, VH // 16), slice(VH // 16, V // 16)]
-        for c, o in zip(halves, lists):
-            nc.vector.tensor_copy(hc[:, c], h[:].indirect(cen_sb[:, o]))
-        for i in range(2):
-            for c, o in zip(halves, lists):
-                nc.vector.tensor_tensor(d[i][:, c], h[:].indirect(pos_sb[i][:, o]), hc[:, c], ALU.subtract)
-        steps = [(i, c) for i in range(2) for c in halves]
+
+        def centre(lo, hi):
+            nc.vector.tensor_copy(hc[:, lo:hi], h[:].indirect(cen_sb[:, lo // 16 : hi // 16]))
+
+        def diff(i, lo, hi):
+            nc.vector.tensor_tensor(d[i][:, lo:hi], h[:].indirect(pos_sb[i][:, lo // 16 : hi // 16]), hc[:, lo:hi], ALU.subtract)
+
+        def square(i, lo, hi):
+            nc.scalar.activation(sq[i][:, lo:hi], d[i][:, lo:hi], ACT.Square)
+
+        def root(i, lo, hi):
+            nc.scalar.activation(r[i][:, lo:hi], sq[i][:, lo:hi], ACT.Abs_reciprocal_sqrt, bias=unit[:])
+
+        def pull(i, lo, hi):
+            nc.vector.scalar_tensor_tensor(t[i][:, lo:hi], d[i][:, lo:hi], rate_sb[:], r[i][:, lo:hi], ALU.mult, ALU.mult)
+
+        def first_sum(lo, hi):
+            nc.vector.tensor_tensor(u[:, lo:hi], t[0][:, lo:hi], hc[:, lo:hi], ALU.add)
+
+        def last_sum(lo, hi):
+            nc.vector.tensor_tensor(res[:, lo:hi], u[:, lo:hi], t[1][:, lo:hi], ALU.add)
+            nc.sync.dma_start(out=out[:, lo:hi], in_=res[:, lo:hi])
+
+        halves = [(0, 128), (128, 256)]
+        thirds = [(0, 128), (128, 192), (192, 256)]
+        for c in halves:
+            centre(*c)
+        for c in halves:
+            diff(0, *c)
+        for c in thirds:
+            diff(1, *c)
+        steps = [(0, *c) for c in halves] + [(1, *c) for c in thirds]
         for k in range(len(steps) + 1):
             if k < len(steps):
-                i, c = steps[k]
-                nc.scalar.activation(sq[i][:, c], d[i][:, c], ACT.Square)
+                square(*steps[k])
             if k > 0:
-                i, c = steps[k - 1]
-                nc.scalar.activation(r[i][:, c], sq[i][:, c], ACT.Abs_reciprocal_sqrt, bias=unit[:])
+                root(*steps[k - 1])
         for c in halves:
-            nc.vector.scalar_tensor_tensor(t[0][:, c], d[0][:, c], rate_sb[:], r[0][:, c], ALU.mult, ALU.mult)
+            pull(0, *c)
         for c in halves:
-            nc.vector.tensor_tensor(u[:, c], t[0][:, c], hc[:, c], ALU.add)
-            nc.vector.scalar_tensor_tensor(t[1][:, c], d[1][:, c], rate_sb[:], r[1][:, c], ALU.mult, ALU.mult)
-        for c in halves:
-            nc.vector.tensor_tensor(res[:, c], u[:, c], t[1][:, c], ALU.add)
-            nc.sync.dma_start(out=out[:, c], in_=res[:, c])
+            first_sum(*c)
+        for k in range(len(thirds) + 1):
+            if k < len(thirds):
+                pull(1, *thirds[k])
+            if k > 0:
+                last_sum(*thirds[k - 1])

@@ -135,26 +135,30 @@ def tile_picked_ypm_tv_p_kernel(tc, x_words, x_scales, w1, rate, offs, cen, pos1
             nc.vector.tensor_tensor(res[:, lo:hi], u[:, lo:hi], t[1][:, lo:hi], ALU.add)
             nc.sync.dma_start(out=out[:, lo:hi], in_=res[:, lo:hi])
 
-        halves = [(0, 128), (128, 256)]
-        thirds = [(0, 128), (128, 192), (192, 256)]
-        for c in halves:
-            centre(*c)
-        for c in halves:
-            diff(0, *c)
-        for c in thirds:
-            diff(1, *c)
-        steps = [(0, *c) for c in halves] + [(1, *c) for c in thirds]
-        for k in range(len(steps) + 1):
-            if k < len(steps):
-                square(*steps[k])
-            if k > 0:
-                root(*steps[k - 1])
-        for c in halves:
-            pull(0, *c)
-        for c in halves:
-            first_sum(*c)
-        for k in range(len(thirds) + 1):
-            if k < len(thirds):
-                pull(1, *thirds[k])
-            if k > 0:
-                last_sum(*thirds[k - 1])
+        centre(0, 128)
+        centre(128, 256)
+        diff(0, 0, 128)
+        diff(1, 0, 128)
+        diff(0, 128, 256)
+        diff(1, 128, 192)
+        diff(1, 192, 256)
+        square(0, 0, 128)
+        square(1, 0, 128)
+        root(0, 0, 128)
+        pull(0, 0, 128)
+        square(0, 128, 256)
+        root(1, 0, 128)
+        pull(1, 0, 128)
+        first_sum(0, 128)
+        root(0, 128, 256)
+        pull(0, 128, 256)
+        last_sum(0, 128)
+        first_sum(128, 256)
+        square(1, 128, 192)
+        square(1, 192, 256)
+        root(1, 128, 192)
+        pull(1, 128, 192)
+        root(1, 192, 256)
+        pull(1, 192, 256)
+        last_sum(128, 192)
+        last_sum(192, 256)

@@ -31,19 +31,19 @@ def tile_picked_ypm_tv_p_kernel(tc, x_words, x_scales, w1, rate, offs, cen, pos1
         offs_sb = keep.tile([P, S // 16], U16, name="offs_sb")
         cen_sb = keep.tile([P, V // 16], U16, name="cen_sb")
         pos_sb = [keep.tile([P, V // 16], U16, name=f"pos_sb{i}") for i in range(2)]
-        scale_table = keep.tile([P, T], U8, name="scale_table", align_bytes=64)
-        word_table = [keep.tile([P, T], U32, name=f"word_table{g}", align_bytes=64) for g in range(PASSES)]
-        w_raw = keep.tile([P, PASSES, PACK, N], F32, name="w_raw")
+        scale_table = keep.tile([P, T], U8, name="scale_table", align_bytes=256)
+        word_table = [keep.tile([P, T], U32, name=f"word_table{g}", align_bytes=256) for g in range(PASSES)]
+        w_raw = keep.tile([P, PASSES, PACK, N], F32, name="w_raw", align_bytes=256)
         ones = keep.tile([P, 1], F32, name="ones")
         unit = keep.tile([P, 1], F32, name="unit")
 
         nc.vector.memset(scale_table[:].bitcast(I32), 0)
         nc.vector.memset(ones[:], 1.0)
-        x_sc = keep.tile([P, S], U8, name="x_sc", align_bytes=64)
+        x_sc = keep.tile([P, S], U8, name="x_sc", align_bytes=256)
 
         nc.sync.dma_start(out=w_raw[:], in_=w1.rearrange("(g p j) m -> p g j m", g=PASSES, j=PACK))
         nc.sync.dma_start(
-            out=scale_table[0:96:3].bitcast(I32),
+            out=scale_table[16:112:3].bitcast(I32),
             in_=x_scales.rearrange("g b t -> b g t").bitcast(I32),
         )
         nc.sync.dma_start(offs_sb[:], offs)
@@ -56,15 +56,15 @@ def tile_picked_ypm_tv_p_kernel(tc, x_words, x_scales, w1, rate, offs, cen, pos1
         nc.sync.dma_start(pos_sb[0][:], pos1)
         nc.sync.dma_start(pos_sb[1][:], pos2)
 
-        picked_sc = keep.tile([P, S], U8, name="picked_sc", tag="picked_sc", align_bytes=64)
+        picked_sc = keep.tile([P, S], U8, name="picked_sc", tag="picked_sc", align_bytes=256)
         nc.vector.tensor_copy(picked_sc[:], scale_table[:].indirect(offs_sb[:]))
         for j in range(4):
             nc.scalar.dma_start(
                 out=x_sc[j:P:4, :].bitcast(I32),
-                in_=picked_sc[6 * j : 6 * j + 96 : 3, :].bitcast(I32),
+                in_=picked_sc[16 + 6 * j : 16 + 6 * j + 94 : 3, :].bitcast(I32),
             )
 
-        rate_sb = keep.tile([P, 1], F32, name="rate_sb", tag="picked_sc", align_bytes=64)
+        rate_sb = keep.tile([P, 1], F32, name="rate_sb", tag="picked_sc", align_bytes=256)
         nc.sync.dma_start(out=rate_sb[:], in_=rate)
 
         nc.scalar.activation(unit[:], ones[:], ACT.Abs_reciprocal_sqrt)
@@ -111,7 +111,7 @@ def tile_picked_ypm_tv_p_kernel(tc, x_words, x_scales, w1, rate, offs, cen, pos1
         r = [keep.tile([P, V], F32, name=f"r{i}") for i in range(2)]
         t = [keep.tile([P, V], F32, name=f"t{i}") for i in range(2)]
         u = keep.tile([P, V], F32, name="u")
-        res = keep.tile([P, V], F32, name="res")
+        res = keep.tile([P, V], F32, name="res", align_bytes=256)
 
         def centre(lo, hi):
             nc.vector.tensor_copy(hc[:, lo:hi], h[:].indirect(cen_sb[:, lo // 16 : hi // 16]))

@@ -65,7 +65,7 @@ def tile_picked_ypm_tv_p_kernel(tc, x_words, x_scales, w1, rate, offs, cen, pos1
             )
 
         rate_sb = keep.tile([P, 1], F32, name="rate_sb", tag="picked_sc", align_bytes=256)
-        nc.sync.dma_start(out=rate_sb[:], in_=rate)
+        nc.scalar.dma_start(out=rate_sb[:], in_=rate)
 
         nc.scalar.activation(unit[:], ones[:], ACT.Abs_reciprocal_sqrt)
 
@@ -131,9 +131,9 @@ def tile_picked_ypm_tv_p_kernel(tc, x_words, x_scales, w1, rate, offs, cen, pos1
         def first_sum(lo, hi):
             nc.vector.tensor_tensor(u[:, lo:hi], t[0][:, lo:hi], hc[:, lo:hi], ALU.add)
 
-        def last_sum(lo, hi):
+        def last_sum(lo, hi, queue=nc.sync):
             nc.vector.tensor_tensor(res[:, lo:hi], u[:, lo:hi], t[1][:, lo:hi], ALU.add)
-            nc.sync.dma_start(out=out[:, lo:hi], in_=res[:, lo:hi])
+            queue.dma_start(out=out[:, lo:hi], in_=res[:, lo:hi])
 
         centre(0, 128)
         centre(128, 256)
@@ -160,5 +160,5 @@ def tile_picked_ypm_tv_p_kernel(tc, x_words, x_scales, w1, rate, offs, cen, pos1
         pull(1, 128, 192)
         root(1, 192, 256)
         pull(1, 192, 256)
-        last_sum(128, 192)
+        last_sum(128, 192, nc.scalar)
         last_sum(192, 256)

@@ -18,8 +18,11 @@ ALU = mybir.AluOpType
 P = 128
 PACK = 4
 PASSES = K // (P * PACK)
-HALF = S // 2
-VH = V // 2
+LANES = 16
+
+
+def entries(list_tile, lo, hi):
+    return list_tile[:, lo // LANES : hi // LANES]
 
 
 def tile_picked_ypm_tv_p_kernel(tc, x_words, x_scales, w1, rate, offs, cen, pos1, pos2, out):
@@ -28,9 +31,9 @@ def tile_picked_ypm_tv_p_kernel(tc, x_words, x_scales, w1, rate, offs, cen, pos1
         keep = ctx.enter_context(tc.tile_pool(name="keep", bufs=1))
         psum = ctx.enter_context(tc.psum_pool(name="psum", bufs=1))
 
-        offs_sb = keep.tile([P, S // 16], U16, name="offs_sb")
-        cen_sb = keep.tile([P, V // 16], U16, name="cen_sb")
-        pos_sb = [keep.tile([P, V // 16], U16, name=f"pos_sb{i}") for i in range(2)]
+        offs_sb = keep.tile([P, S // LANES], U16, name="offs_sb")
+        cen_sb = keep.tile([P, V // LANES], U16, name="cen_sb")
+        pos_sb = [keep.tile([P, V // LANES], U16, name=f"pos_sb{i}") for i in range(2)]
         scale_table = keep.tile([P, T], U8, name="scale_table", align_bytes=256)
         word_table = [keep.tile([P, T], U32, name=f"word_table{g}", align_bytes=256) for g in range(PASSES)]
         w_raw = keep.tile([P, PASSES, PACK, N], F32, name="w_raw", align_bytes=256)
@@ -80,17 +83,15 @@ def tile_picked_ypm_tv_p_kernel(tc, x_words, x_scales, w1, rate, offs, cen, pos1
             in_=w_bf[:].rearrange("p g m j -> p (g m j)"),
         )
 
-
         h = keep.tile([P, S], F32, name="h", align_bytes=64)
+        HALF = S // 2
         QUART = HALF // 2
         spans = [[(0, HALF)], [(HALF, QUART), (HALF + QUART, QUART)]]
         acc = {lo: psum.tile([P, n], F32, name=f"acc{lo}") for span in spans for lo, n in span}
         for g in range(PASSES):
             for a in range(2):
                 x_codes = keep.tile([P, HALF], U32, name=f"x_codes{g}{a}", align_bytes=64)
-                nc.vector.tensor_copy(
-                    x_codes[:], word_table[g][:].indirect(offs_sb[:, a * HALF // 16 : (a + 1) * HALF // 16])
-                )
+                nc.vector.tensor_copy(x_codes[:], word_table[g][:].indirect(entries(offs_sb, a * HALF, (a + 1) * HALF)))
                 for lo, n in spans[a]:
                     nc.tensor.matmul_mx(
                         out=acc[lo][:],
@@ -105,7 +106,9 @@ def tile_picked_ypm_tv_p_kernel(tc, x_words, x_scales, w1, rate, offs, cen, pos1
         nc.vector.tensor_copy(out=h[:, HALF : HALF + QUART], in_=acc[HALF][:])
         nc.scalar.copy(out=h[:, HALF + QUART :], in_=acc[HALF + QUART][:])
 
+
         hc = keep.tile([P, V], F32, name="hc")
+        g = [keep.tile([P, V], F32, name=f"g{i}") for i in range(2)]
         d = [keep.tile([P, V], F32, name=f"d{i}") for i in range(2)]
         sq = [keep.tile([P, V], F32, name=f"sq{i}") for i in range(2)]
         r = [keep.tile([P, V], F32, name=f"r{i}") for i in range(2)]
@@ -113,14 +116,29 @@ def tile_picked_ypm_tv_p_kernel(tc, x_words, x_scales, w1, rate, offs, cen, pos1
         u = keep.tile([P, V], F32, name="u")
         res = keep.tile([P, V], F32, name="res", align_bytes=256)
 
-        def centre(lo, hi):
-            nc.vector.tensor_copy(hc[:, lo:hi], h[:].indirect(cen_sb[:, lo // 16 : hi // 16]))
+        def centre_s(lo, hi):
+            nc.scalar.activation(hc[:, lo:hi], h[:].indirect(entries(cen_sb, lo, hi)), ACT.Copy)
+
+        def centre_v(lo, hi):
+            nc.vector.tensor_copy(hc[:, lo:hi], h[:].indirect(entries(cen_sb, lo, hi)))
+
+        def fetch_s(i, lo, hi):
+            nc.scalar.activation(g[i][:, lo:hi], h[:].indirect(entries(pos_sb[i], lo, hi)), ACT.Copy)
+
+        def fetch_v(i, lo, hi):
+            nc.vector.tensor_copy(g[i][:, lo:hi], h[:].indirect(entries(pos_sb[i], lo, hi)))
+
+        def sub(i, lo, hi):
+            nc.vector.tensor_tensor(d[i][:, lo:hi], g[i][:, lo:hi], hc[:, lo:hi], ALU.subtract)
 
         def diff(i, lo, hi):
-            nc.vector.tensor_tensor(d[i][:, lo:hi], h[:].indirect(pos_sb[i][:, lo // 16 : hi // 16]), hc[:, lo:hi], ALU.subtract)
+            nc.vector.tensor_tensor(d[i][:, lo:hi], h[:].indirect(entries(pos_sb[i], lo, hi)), hc[:, lo:hi], ALU.subtract)
 
         def square(i, lo, hi):
             nc.scalar.activation(sq[i][:, lo:hi], d[i][:, lo:hi], ACT.Square)
+
+        def square_v(i, lo, hi):
+            nc.vector.tensor_tensor(sq[i][:, lo:hi], d[i][:, lo:hi], d[i][:, lo:hi], ALU.mult)
 
         def root(i, lo, hi):
             nc.scalar.activation(r[i][:, lo:hi], sq[i][:, lo:hi], ACT.Abs_reciprocal_sqrt, bias=unit[:])
@@ -135,30 +153,30 @@ def tile_picked_ypm_tv_p_kernel(tc, x_words, x_scales, w1, rate, offs, cen, pos1
             nc.vector.tensor_tensor(res[:, lo:hi], u[:, lo:hi], t[1][:, lo:hi], ALU.add)
             queue.dma_start(out=out[:, lo:hi], in_=res[:, lo:hi])
 
-        centre(0, 128)
-        centre(128, 256)
+        centre_v(0, 128)
+        centre_s(128, 256)
+        fetch_v(0, 128, 256)
+        fetch_s(1, 128, 256)
         diff(0, 0, 128)
         diff(1, 0, 128)
-        diff(0, 128, 256)
-        diff(1, 128, 192)
-        diff(1, 192, 256)
+        sub(0, 128, 256)
+        sub(1, 128, 256)
         square(0, 0, 128)
         square(1, 0, 128)
         root(0, 0, 128)
-        pull(0, 0, 128)
-        square(0, 128, 256)
         root(1, 0, 128)
+        square_v(0, 128, 256)
+        square_v(1, 128, 256)
+        root(0, 128, 256)
+        root(1, 128, 192)
+        root(1, 192, 256)
+        pull(0, 0, 128)
         pull(1, 0, 128)
         first_sum(0, 128)
-        root(0, 128, 256)
         pull(0, 128, 256)
-        last_sum(0, 128)
         first_sum(128, 256)
-        square(1, 128, 192)
-        square(1, 192, 256)
-        root(1, 128, 192)
+        last_sum(0, 128)
         pull(1, 128, 192)
-        root(1, 192, 256)
         pull(1, 192, 256)
         last_sum(128, 192, nc.scalar)
         last_sum(192, 256)

@@ -84,27 +84,26 @@ def tile_picked_ypm_tv_p_kernel(tc, x_words, x_scales, w1, rate, offs, cen, pos1
         )
 
         h = keep.tile([P, S], F32, name="h", align_bytes=64)
-        HALF = S // 2
-        QUART = HALF // 2
-        spans = [[(0, HALF)], [(HALF, QUART), (HALF + QUART, QUART)]]
-        acc = {lo: psum.tile([P, n], F32, name=f"acc{lo}") for span in spans for lo, n in span}
+        spans = [(0, 256), (256, 384), (384, 512)]
+        acc = [psum.tile([P, hi - lo], F32, name=f"acc{lo}") for lo, hi in spans]
+        cuts = [[(0, 256), (256, 512)], spans]
         for g in range(PASSES):
-            for a in range(2):
-                x_codes = keep.tile([P, HALF], U32, name=f"x_codes{g}{a}", align_bytes=64)
-                nc.vector.tensor_copy(x_codes[:], word_table[g][:].indirect(entries(offs_sb, a * HALF, (a + 1) * HALF)))
-                for lo, n in spans[a]:
-                    nc.tensor.matmul_mx(
-                        out=acc[lo][:],
-                        lhsT=w_codes[:, g * N : (g + 1) * N].bitcast(FP8X4),
-                        lhsT_scale=w_scales[:, g * N : (g + 1) * N],
-                        rhs=x_codes[:, lo - a * HALF : lo - a * HALF + n].bitcast(FP8X4),
-                        rhs_scale=x_sc[4 * g :, lo : lo + n],
-                        start=(g == 0),
-                        stop=(g == PASSES - 1),
-                    )
-        nc.scalar.copy(out=h[:, :HALF], in_=acc[0][:])
-        nc.vector.tensor_copy(out=h[:, HALF : HALF + QUART], in_=acc[HALF][:])
-        nc.scalar.copy(out=h[:, HALF + QUART :], in_=acc[HALF + QUART][:])
+            x_codes = keep.tile([P, S], U32, name=f"x_codes{g}", align_bytes=64)
+            for lo, hi in cuts[g]:
+                nc.vector.tensor_copy(x_codes[:, lo:hi], word_table[g][:].indirect(entries(offs_sb, lo, hi)))
+            for bank, (lo, hi) in zip(acc, spans):
+                nc.tensor.matmul_mx(
+                    out=bank[:],
+                    lhsT=w_codes[:, g * N : (g + 1) * N].bitcast(FP8X4),
+                    lhsT_scale=w_scales[:, g * N : (g + 1) * N],
+                    rhs=x_codes[:, lo:hi].bitcast(FP8X4),
+                    rhs_scale=x_sc[4 * g :, lo:hi],
+                    start=(g == 0),
+                    stop=(g == PASSES - 1),
+                )
+        nc.scalar.copy(out=h[:, 0:256], in_=acc[0][:])
+        nc.scalar.copy(out=h[:, 256:384], in_=acc[1][:])
+        nc.vector.tensor_copy(out=h[:, 384:512], in_=acc[2][:])
 
 
         hc = keep.tile([P, V], F32, name="hc")
@@ -155,10 +154,11 @@ def tile_picked_ypm_tv_p_kernel(tc, x_words, x_scales, w1, rate, offs, cen, pos1
 
         centre_v(0, 128)
         centre_s(128, 256)
-        fetch_v(0, 128, 256)
+        fetch_s(0, 128, 256)
         fetch_s(1, 128, 256)
+        fetch_v(1, 0, 128)
         diff(0, 0, 128)
-        diff(1, 0, 128)
+        sub(1, 0, 128)
         sub(0, 128, 256)
         sub(1, 128, 256)
         square(0, 0, 128)
@@ -168,15 +168,13 @@ def tile_picked_ypm_tv_p_kernel(tc, x_words, x_scales, w1, rate, offs, cen, pos1
         square_v(0, 128, 256)
         square_v(1, 128, 256)
         root(0, 128, 256)
-        root(1, 128, 192)
-        root(1, 192, 256)
+        root(1, 128, 256)
         pull(0, 0, 128)
         pull(1, 0, 128)
         first_sum(0, 128)
         pull(0, 128, 256)
         first_sum(128, 256)
         last_sum(0, 128)
-        pull(1, 128, 192)
-        pull(1, 192, 256)
+        pull(1, 128, 256)
         last_sum(128, 192, nc.scalar)
         last_sum(192, 256)

@@ -106,75 +106,89 @@ def tile_picked_ypm_tv_p_kernel(tc, x_words, x_scales, w1, rate, offs, cen, pos1
         nc.vector.tensor_copy(out=h[:, 384:512], in_=acc[2][:])
 
 
-        hc = keep.tile([P, V], F32, name="hc")
-        g = [keep.tile([P, V], F32, name=f"g{i}") for i in range(2)]
-        d = [keep.tile([P, V], F32, name=f"d{i}") for i in range(2)]
-        sq = [keep.tile([P, V], F32, name=f"sq{i}") for i in range(2)]
-        r = [keep.tile([P, V], F32, name=f"r{i}") for i in range(2)]
-        t = [keep.tile([P, V], F32, name=f"t{i}") for i in range(2)]
-        u = keep.tile([P, V], F32, name="u")
-        res = keep.tile([P, V], F32, name="res", align_bytes=256)
+        half = V // 2
+
+        def halves(name, **kw):
+            return [keep.tile([P, half], F32, name=f"{name}{a}", **kw) for a in range(2)]
+
+        def cut(tiles, lo, hi):
+            return tiles[lo // half][:, lo % half : lo % half + hi - lo]
+
+        hc = halves("hc")
+        nb = [halves(f"nb{i}") for i in range(2)]
+        d = [halves(f"d{i}") for i in range(2)]
+        sq = [halves(f"sq{i}") for i in range(2)]
+        r = [halves(f"r{i}") for i in range(2)]
+        t = [halves(f"t{i}") for i in range(2)]
+        u = halves("u")
+        res = halves("res", align_bytes=256)
 
         def centre_s(lo, hi):
-            nc.scalar.activation(hc[:, lo:hi], h[:].indirect(entries(cen_sb, lo, hi)), ACT.Copy)
+            nc.scalar.activation(cut(hc, lo, hi), h[:].indirect(entries(cen_sb, lo, hi)), ACT.Copy)
 
         def centre_v(lo, hi):
-            nc.vector.tensor_copy(hc[:, lo:hi], h[:].indirect(entries(cen_sb, lo, hi)))
+            nc.vector.tensor_copy(cut(hc, lo, hi), h[:].indirect(entries(cen_sb, lo, hi)))
 
         def fetch_s(i, lo, hi):
-            nc.scalar.activation(g[i][:, lo:hi], h[:].indirect(entries(pos_sb[i], lo, hi)), ACT.Copy)
+            nc.scalar.activation(cut(nb[i], lo, hi), h[:].indirect(entries(pos_sb[i], lo, hi)), ACT.Copy)
 
         def fetch_v(i, lo, hi):
-            nc.vector.tensor_copy(g[i][:, lo:hi], h[:].indirect(entries(pos_sb[i], lo, hi)))
+            nc.vector.tensor_copy(cut(nb[i], lo, hi), h[:].indirect(entries(pos_sb[i], lo, hi)))
 
         def sub(i, lo, hi):
-            nc.vector.tensor_tensor(d[i][:, lo:hi], g[i][:, lo:hi], hc[:, lo:hi], ALU.subtract)
+            nc.vector.tensor_tensor(cut(d[i], lo, hi), cut(nb[i], lo, hi), cut(hc, lo, hi), ALU.subtract)
 
         def diff(i, lo, hi):
-            nc.vector.tensor_tensor(d[i][:, lo:hi], h[:].indirect(entries(pos_sb[i], lo, hi)), hc[:, lo:hi], ALU.subtract)
+            nc.vector.tensor_tensor(
+                cut(d[i], lo, hi), h[:].indirect(entries(pos_sb[i], lo, hi)), cut(hc, lo, hi), ALU.subtract
+            )
 
         def square(i, lo, hi):
-            nc.scalar.activation(sq[i][:, lo:hi], d[i][:, lo:hi], ACT.Square)
+            nc.scalar.activation(cut(sq[i], lo, hi), cut(d[i], lo, hi), ACT.Square)
 
         def square_v(i, lo, hi):
-            nc.vector.tensor_tensor(sq[i][:, lo:hi], d[i][:, lo:hi], d[i][:, lo:hi], ALU.mult)
+            nc.vector.tensor_tensor(cut(sq[i], lo, hi), cut(d[i], lo, hi), cut(d[i], lo, hi), ALU.mult)
 
         def root(i, lo, hi):
-            nc.scalar.activation(r[i][:, lo:hi], sq[i][:, lo:hi], ACT.Abs_reciprocal_sqrt, bias=unit[:])
+            nc.scalar.activation(cut(r[i], lo, hi), cut(sq[i], lo, hi), ACT.Abs_reciprocal_sqrt, bias=unit[:])
 
         def pull(i, lo, hi):
-            nc.vector.scalar_tensor_tensor(t[i][:, lo:hi], d[i][:, lo:hi], rate_sb[:], r[i][:, lo:hi], ALU.mult, ALU.mult)
+            nc.vector.scalar_tensor_tensor(
+                cut(t[i], lo, hi), cut(d[i], lo, hi), rate_sb[:], cut(r[i], lo, hi), ALU.mult, ALU.mult
+            )
 
         def first_sum(lo, hi):
-            nc.vector.tensor_tensor(u[:, lo:hi], t[0][:, lo:hi], hc[:, lo:hi], ALU.add)
+            nc.vector.tensor_tensor(cut(u, lo, hi), cut(t[0], lo, hi), cut(hc, lo, hi), ALU.add)
 
         def last_sum(lo, hi, queue=nc.sync):
-            nc.vector.tensor_tensor(res[:, lo:hi], u[:, lo:hi], t[1][:, lo:hi], ALU.add)
-            queue.dma_start(out=out[:, lo:hi], in_=res[:, lo:hi])
+            nc.vector.tensor_tensor(cut(res, lo, hi), cut(u, lo, hi), cut(t[1], lo, hi), ALU.add)
+            queue.dma_start(out=out[:, lo:hi], in_=cut(res, lo, hi))
 
         centre_v(0, 128)
         centre_s(128, 256)
-        fetch_s(0, 128, 256)
+        fetch_v(0, 128, 256)
+        fetch_s(1, 0, 128)
         fetch_s(1, 128, 256)
-        fetch_v(1, 0, 128)
         diff(0, 0, 128)
-        sub(1, 0, 128)
         sub(0, 128, 256)
+        sub(1, 0, 128)
+
         sub(1, 128, 256)
         square(0, 0, 128)
-        square(1, 0, 128)
+        square(0, 128, 256)
         root(0, 0, 128)
-        root(1, 0, 128)
-        square_v(0, 128, 256)
-        square_v(1, 128, 256)
         root(0, 128, 256)
+        square_v(1, 0, 128)
+        square_v(1, 128, 256)
+        root(1, 0, 128)
         root(1, 128, 256)
         pull(0, 0, 128)
-        pull(1, 0, 128)
-        first_sum(0, 128)
         pull(0, 128, 256)
+        first_sum(0, 128)
+        pull(1, 0, 128)
         first_sum(128, 256)
+        pull(1, 128, 192)
+        pull(1, 192, 256)
         last_sum(0, 128)
-        pull(1, 128, 256)
         last_sum(128, 192, nc.scalar)
         last_sum(192, 256)

@@ -103,7 +103,7 @@ def tile_picked_ypm_tv_p_kernel(tc, x_words, x_scales, w1, rate, offs, cen, pos1
                 )
         nc.scalar.copy(out=h[:, 0:256], in_=acc[0][:])
         nc.scalar.copy(out=h[:, 256:384], in_=acc[1][:])
-        nc.vector.tensor_copy(out=h[:, 384:512], in_=acc[2][:])
+        nc.scalar.copy(out=h[:, 384:512], in_=acc[2][:])
 
 
         half = V // 2

@@ -19,13 +19,29 @@ P = 128
 PACK = 4
 PASSES = K // (P * PACK)
 LANES = 16
+DMA_ALIGN = 256
+MX_ALIGN = 64
+
+ROW0, ROW_STEP = 16, 3
+SCALE_ROWS = K // 32
+
+BANKS = [(0, S // 2), (S // 2, 3 * S // 4), (3 * S // 4, S)]
+
+HALF, QUARTER = V // 2, V // 4
+EARLY, LATE = (0, HALF), (HALF, V)
 
 
-def entries(list_tile, lo, hi):
-    return list_tile[:, lo // LANES : hi // LANES]
+def entries(list_tile, span):
+    return list_tile[:, span[0] // LANES : span[1] // LANES]
 
 
-def tile_picked_ypm_tv_p_kernel(tc, x_words, x_scales, w1, rate, offs, cen, pos1, pos2, out):
+def quarters(span):
+    return [(lo, lo + QUARTER) for lo in range(span[0], span[1], QUARTER)]
+
+
+def tile_picked_ypm_tv_p_kernel(
+    tc, x_words, x_scales, w1, rate, offs, cen, pos1, pos2, out
+):
     nc = tc.nc
     with ExitStack() as ctx:
         keep = ctx.enter_context(tc.tile_pool(name="keep", bufs=1))
@@ -34,19 +50,19 @@ def tile_picked_ypm_tv_p_kernel(tc, x_words, x_scales, w1, rate, offs, cen, pos1
         offs_sb = keep.tile([P, S // LANES], U16, name="offs_sb")
         cen_sb = keep.tile([P, V // LANES], U16, name="cen_sb")
         pos_sb = [keep.tile([P, V // LANES], U16, name=f"pos_sb{i}") for i in range(2)]
-        scale_table = keep.tile([P, T], U8, name="scale_table", align_bytes=256)
-        word_table = [keep.tile([P, T], U32, name=f"word_table{g}", align_bytes=256) for g in range(PASSES)]
-        w_raw = keep.tile([P, PASSES, PACK, N], F32, name="w_raw", align_bytes=256)
+        scale_table = keep.tile([P, T], U8, name="scale_table", align_bytes=DMA_ALIGN)
+        word_table = [keep.tile([P, T], U32, name=f"word_table{g}", align_bytes=DMA_ALIGN) for g in range(PASSES)]
+        w_raw = keep.tile([P, PASSES, PACK, N], F32, name="w_raw", align_bytes=DMA_ALIGN)
         ones = keep.tile([P, 1], F32, name="ones")
         unit = keep.tile([P, 1], F32, name="unit")
 
         nc.vector.memset(scale_table[:].bitcast(I32), 0)
         nc.vector.memset(ones[:], 1.0)
-        x_sc = keep.tile([P, S], U8, name="x_sc", align_bytes=256)
+        x_scale = keep.tile([P, S], U8, name="x_sc", align_bytes=DMA_ALIGN)
 
         nc.sync.dma_start(out=w_raw[:], in_=w1.rearrange("(g p j) m -> p g j m", g=PASSES, j=PACK))
         nc.sync.dma_start(
-            out=scale_table[16:112:3].bitcast(I32),
+            out=scale_table[ROW0 : ROW0 + ROW_STEP * SCALE_ROWS : ROW_STEP].bitcast(I32),
             in_=x_scales.rearrange("g b t -> b g t").bitcast(I32),
         )
         nc.sync.dma_start(offs_sb[:], offs)
@@ -59,136 +75,109 @@ def tile_picked_ypm_tv_p_kernel(tc, x_words, x_scales, w1, rate, offs, cen, pos1
         nc.sync.dma_start(pos_sb[0][:], pos1)
         nc.sync.dma_start(pos_sb[1][:], pos2)
 
-        picked_sc = keep.tile([P, S], U8, name="picked_sc", tag="picked_sc", align_bytes=256)
-        nc.vector.tensor_copy(picked_sc[:], scale_table[:].indirect(offs_sb[:]))
-        for j in range(4):
+        picked_scale = keep.tile([P, S], U8, name="picked_sc", tag="picked_sc", align_bytes=DMA_ALIGN)
+        nc.vector.tensor_copy(picked_scale[:], scale_table[:].indirect(offs_sb[:]))
+        for j in range(PACK):
+            first = ROW0 + ROW_STEP * 2 * j
             nc.scalar.dma_start(
-                out=x_sc[j:P:4, :].bitcast(I32),
-                in_=picked_sc[16 + 6 * j : 16 + 6 * j + 94 : 3, :].bitcast(I32),
+                out=x_scale[j:P:PACK, :].bitcast(I32),
+                in_=picked_scale[first : first + ROW_STEP * (SCALE_ROWS - 1) + 1 : ROW_STEP, :].bitcast(I32),
             )
 
-        rate_sb = keep.tile([P, 1], F32, name="rate_sb", tag="picked_sc", align_bytes=256)
+        rate_sb = keep.tile([P, 1], F32, name="rate_sb", tag="picked_sc", align_bytes=DMA_ALIGN)
         nc.scalar.dma_start(out=rate_sb[:], in_=rate)
 
         nc.scalar.activation(unit[:], ones[:], ACT.Abs_reciprocal_sqrt)
 
-        w_bf = keep.tile([P, PASSES, N, PACK], BF16, name="w_bf", align_bytes=64)
+        w_bf = keep.tile([P, PASSES, N, PACK], BF16, name="w_bf", align_bytes=MX_ALIGN)
         for g in range(PASSES):
             nc.scalar.copy(out=w_bf[:, g], in_=w_raw[:, g].rearrange("p j m -> p m j"))
-        w_codes = keep.tile([P, PASSES * N], U32, name="w_codes", align_bytes=64)
-        w_scales = keep.tile([P, PASSES * N], U8, name="w_scales", align_bytes=64)
+        w_codes = keep.tile([P, PASSES * N], U32, name="w_codes", align_bytes=MX_ALIGN)
+        w_scale = keep.tile([P, PASSES * N], U8, name="w_scales", align_bytes=MX_ALIGN)
         nc.vector.quantize_mx(
             out=w_codes[:].bitcast(FP8X4),
-            scales=w_scales[:],
+            scales=w_scale[:],
             in_=w_bf[:].rearrange("p g m j -> p (g m j)"),
         )
 
-        h = keep.tile([P, S], F32, name="h", align_bytes=64)
-        spans = [(0, 256), (256, 384), (384, 512)]
-        acc = [psum.tile([P, hi - lo], F32, name=f"acc{lo}") for lo, hi in spans]
-        cuts = [[(0, 256), (256, 512)], spans]
+        h = keep.tile([P, S], F32, name="h", align_bytes=MX_ALIGN)
+        acc = [psum.tile([P, hi - lo], F32, name=f"acc{lo}") for lo, hi in BANKS]
+        gather_spans = [[(0, S // 2), (S // 2, S)], BANKS]
         for g in range(PASSES):
-            x_codes = keep.tile([P, S], U32, name=f"x_codes{g}", align_bytes=64)
-            for lo, hi in cuts[g]:
-                nc.vector.tensor_copy(x_codes[:, lo:hi], word_table[g][:].indirect(entries(offs_sb, lo, hi)))
-            for bank, (lo, hi) in zip(acc, spans):
+            x_codes = keep.tile([P, S], U32, name=f"x_codes{g}", align_bytes=MX_ALIGN)
+            for lo, hi in gather_spans[g]:
+                nc.vector.tensor_copy(x_codes[:, lo:hi], word_table[g][:].indirect(entries(offs_sb, (lo, hi))))
+            for bank, (lo, hi) in zip(acc, BANKS):
                 nc.tensor.matmul_mx(
                     out=bank[:],
                     lhsT=w_codes[:, g * N : (g + 1) * N].bitcast(FP8X4),
-                    lhsT_scale=w_scales[:, g * N : (g + 1) * N],
+                    lhsT_scale=w_scale[:, g * N : (g + 1) * N],
                     rhs=x_codes[:, lo:hi].bitcast(FP8X4),
-                    rhs_scale=x_sc[4 * g :, lo:hi],
+                    rhs_scale=x_scale[PACK * g :, lo:hi],
                     start=(g == 0),
                     stop=(g == PASSES - 1),
                 )
-        nc.scalar.copy(out=h[:, 0:256], in_=acc[0][:])
-        nc.scalar.copy(out=h[:, 256:384], in_=acc[1][:])
-        nc.scalar.copy(out=h[:, 384:512], in_=acc[2][:])
+        for bank, (lo, hi) in zip(acc, BANKS):
+            nc.scalar.copy(out=h[:, lo:hi], in_=bank[:])
 
+        def by_halves(name, **options):
+            return [keep.tile([P, HALF], F32, name=f"{name}{a}", **options) for a in range(2)]
 
-        half = V // 2
+        def cut(halves, span):
+            lo, hi = span
+            return halves[lo // HALF][:, lo % HALF : lo % HALF + hi - lo]
 
-        def halves(name, **kw):
-            return [keep.tile([P, half], F32, name=f"{name}{a}", **kw) for a in range(2)]
+        centre = by_halves("hc")
+        first_late = keep.tile([P, HALF], F32, name="nb01")
+        second = by_halves("nb1")
+        diff = [by_halves(f"d{i}") for i in range(2)]
+        square = [by_halves(f"sq{i}") for i in range(2)]
+        damp = [by_halves(f"r{i}") for i in range(2)]
+        pull = [by_halves(f"t{i}") for i in range(2)]
+        part = by_halves("u")
+        res = by_halves("res", align_bytes=DMA_ALIGN)
 
-        def cut(tiles, lo, hi):
-            return tiles[lo // half][:, lo % half : lo % half + hi - lo]
+        def look_up(list_tile, span):
+            return h[:].indirect(entries(list_tile, span))
 
-        hc = halves("hc")
-        nb = [halves(f"nb{i}") for i in range(2)]
-        d = [halves(f"d{i}") for i in range(2)]
-        sq = [halves(f"sq{i}") for i in range(2)]
-        r = [halves(f"r{i}") for i in range(2)]
-        t = [halves(f"t{i}") for i in range(2)]
-        u = halves("u")
-        res = halves("res", align_bytes=256)
+        def root(i, span):
+            nc.scalar.activation(cut(damp[i], span), cut(square[i], span), ACT.Abs_reciprocal_sqrt, bias=unit[:])
 
-        def centre_s(lo, hi):
-            nc.scalar.activation(cut(hc, lo, hi), h[:].indirect(entries(cen_sb, lo, hi)), ACT.Copy)
-
-        def centre_v(lo, hi):
-            nc.vector.tensor_copy(cut(hc, lo, hi), h[:].indirect(entries(cen_sb, lo, hi)))
-
-        def fetch_s(i, lo, hi):
-            nc.scalar.activation(cut(nb[i], lo, hi), h[:].indirect(entries(pos_sb[i], lo, hi)), ACT.Copy)
-
-        def fetch_v(i, lo, hi):
-            nc.vector.tensor_copy(cut(nb[i], lo, hi), h[:].indirect(entries(pos_sb[i], lo, hi)))
-
-        def sub(i, lo, hi):
-            nc.vector.tensor_tensor(cut(d[i], lo, hi), cut(nb[i], lo, hi), cut(hc, lo, hi), ALU.subtract)
-
-        def diff(i, lo, hi):
-            nc.vector.tensor_tensor(
-                cut(d[i], lo, hi), h[:].indirect(entries(pos_sb[i], lo, hi)), cut(hc, lo, hi), ALU.subtract
-            )
-
-        def square(i, lo, hi):
-            nc.scalar.activation(cut(sq[i], lo, hi), cut(d[i], lo, hi), ACT.Square)
-
-        def square_v(i, lo, hi):
-            nc.vector.tensor_tensor(cut(sq[i], lo, hi), cut(d[i], lo, hi), cut(d[i], lo, hi), ALU.mult)
-
-        def root(i, lo, hi):
-            nc.scalar.activation(cut(r[i], lo, hi), cut(sq[i], lo, hi), ACT.Abs_reciprocal_sqrt, bias=unit[:])
-
-        def pull(i, lo, hi):
+        def product(i, span):
             nc.vector.scalar_tensor_tensor(
-                cut(t[i], lo, hi), cut(d[i], lo, hi), rate_sb[:], cut(r[i], lo, hi), ALU.mult, ALU.mult
+                cut(pull[i], span), cut(diff[i], span), rate_sb[:], cut(damp[i], span), ALU.mult, ALU.mult
             )
 
-        def first_sum(lo, hi):
-            nc.vector.tensor_tensor(cut(u, lo, hi), cut(t[0], lo, hi), cut(hc, lo, hi), ALU.add)
+        def first_sum(span):
+            nc.vector.tensor_tensor(cut(part, span), cut(pull[0], span), cut(centre, span), ALU.add)
 
-        def last_sum(lo, hi, queue=nc.sync):
-            nc.vector.tensor_tensor(cut(res, lo, hi), cut(u, lo, hi), cut(t[1], lo, hi), ALU.add)
-            queue.dma_start(out=out[:, lo:hi], in_=cut(res, lo, hi))
+        nc.vector.tensor_copy(cut(centre, EARLY), look_up(cen_sb, EARLY))
+        nc.scalar.activation(cut(centre, LATE), look_up(cen_sb, LATE), ACT.Copy)
+        nc.vector.tensor_copy(first_late[:], look_up(pos_sb[0], LATE))
+        for span in (EARLY, LATE):
+            nc.scalar.activation(cut(second, span), look_up(pos_sb[1], span), ACT.Copy)
+        nc.vector.tensor_tensor(cut(diff[0], EARLY), look_up(pos_sb[0], EARLY), cut(centre, EARLY), ALU.subtract)
+        nc.vector.tensor_tensor(cut(diff[0], LATE), first_late[:], cut(centre, LATE), ALU.subtract)
+        for span in (EARLY, LATE):
+            nc.vector.tensor_tensor(cut(diff[1], span), cut(second, span), cut(centre, span), ALU.subtract)
 
-        centre_v(0, 128)
-        centre_s(128, 256)
-        fetch_v(0, 128, 256)
-        fetch_s(1, 0, 128)
-        fetch_s(1, 128, 256)
-        diff(0, 0, 128)
-        sub(0, 128, 256)
-        sub(1, 0, 128)
+        first_spans = quarters(EARLY) + [LATE]
+        for span in first_spans:
+            nc.scalar.activation(cut(square[0], span), cut(diff[0], span), ACT.Square)
+        for span in first_spans:
+            root(0, span)
+        for span in (EARLY, LATE):
+            nc.vector.tensor_tensor(cut(square[1], span), cut(diff[1], span), cut(diff[1], span), ALU.mult)
+        for span in (EARLY, LATE):
+            root(1, span)
 
-        sub(1, 128, 256)
-        square(0, 0, 128)
-        square(0, 128, 256)
-        root(0, 0, 128)
-        root(0, 128, 256)
-        square_v(1, 0, 128)
-        square_v(1, 128, 256)
-        root(1, 0, 128)
-        root(1, 128, 256)
-        pull(0, 0, 128)
-        pull(0, 128, 256)
-        first_sum(0, 128)
-        pull(1, 0, 128)
-        first_sum(128, 256)
-        pull(1, 128, 192)
-        pull(1, 192, 256)
-        last_sum(0, 128)
-        last_sum(128, 192, nc.scalar)
-        last_sum(192, 256)
+        for span in first_spans:
+            product(0, span)
+        first_sum(EARLY)
+        product(1, EARLY)
+        first_sum(LATE)
+        for span in quarters(LATE):
+            product(1, span)
+        for span, queue in zip([EARLY] + quarters(LATE), (nc.sync, nc.scalar, nc.sync)):
+            nc.vector.tensor_tensor(cut(res, span), cut(part, span), cut(pull[1], span), ALU.add)
+            queue.dma_start(out=out[:, span[0] : span[1]], in_=cut(res, span))

@@ -52,7 +52,7 @@ def tile_picked_ypm_tv_p_kernel(
         pos_sb = [keep.tile([P, V // LANES], U16, name=f"pos_sb{i}") for i in range(2)]
         scale_table = keep.tile([P, T], U8, name="scale_table", align_bytes=DMA_ALIGN)
         word_table = [keep.tile([P, T], U32, name=f"word_table{g}", align_bytes=DMA_ALIGN) for g in range(PASSES)]
-        w_raw = keep.tile([P, PASSES, PACK, N], F32, name="w_raw", align_bytes=DMA_ALIGN)
+        w_raw = keep.tile([P, PASSES, PACK, N], F32, name="w_raw", tag="w_raw", align_bytes=DMA_ALIGN)
         ones = keep.tile([P, 1], F32, name="ones")
         unit = keep.tile([P, 1], F32, name="unit")
 
@@ -75,7 +75,7 @@ def tile_picked_ypm_tv_p_kernel(
         nc.sync.dma_start(pos_sb[0][:], pos1)
         nc.sync.dma_start(pos_sb[1][:], pos2)
 
-        picked_scale = keep.tile([P, S], U8, name="picked_sc", tag="picked_sc", align_bytes=DMA_ALIGN)
+        picked_scale = keep.tile([P, S], U8, name="picked_sc", align_bytes=DMA_ALIGN)
         nc.vector.tensor_copy(picked_scale[:], scale_table[:].indirect(offs_sb[:]))
         for j in range(PACK):
             first = ROW0 + ROW_STEP * 2 * j
@@ -84,14 +84,15 @@ def tile_picked_ypm_tv_p_kernel(
                 in_=picked_scale[first : first + ROW_STEP * (SCALE_ROWS - 1) + 1 : ROW_STEP, :].bitcast(I32),
             )
 
-        rate_sb = keep.tile([P, 1], F32, name="rate_sb", tag="picked_sc", align_bytes=DMA_ALIGN)
-        nc.scalar.dma_start(out=rate_sb[:], in_=rate)
-
         nc.scalar.activation(unit[:], ones[:], ACT.Abs_reciprocal_sqrt)
 
         w_bf = keep.tile([P, PASSES, N, PACK], BF16, name="w_bf", align_bytes=MX_ALIGN)
         for g in range(PASSES):
             nc.scalar.copy(out=w_bf[:, g], in_=w_raw[:, g].rearrange("p j m -> p m j"))
+
+        rate_sb = keep.tile([P, 1], F32, name="rate_sb", tag="w_raw", align_bytes=DMA_ALIGN)
+        nc.scalar.dma_start(out=rate_sb[:], in_=rate)
+
         w_codes = keep.tile([P, PASSES * N], U32, name="w_codes", align_bytes=MX_ALIGN)
         w_scale = keep.tile([P, PASSES * N], U8, name="w_scales", align_bytes=MX_ALIGN)
         nc.vector.quantize_mx(

@@ -121,25 +121,35 @@ def tile_picked_ypm_tv_p_kernel(
         for bank, (lo, hi) in zip(acc, BANKS):
             nc.scalar.copy(out=h[:, lo:hi], in_=bank[:])
 
-        def by_halves(name, **options):
-            return [keep.tile([P, HALF], F32, name=f"{name}{a}", **options) for a in range(2)]
+        def tile_of(name, **options):
+            return keep.tile([P, V], F32, name=name, **options)
 
-        def cut(halves, span):
-            lo, hi = span
-            return halves[lo // HALF][:, lo % HALF : lo % HALF + hi - lo]
+        centre = tile_of("hc")
+        fetched = [tile_of(f"nb{i}") for i in range(2)]
+        diff = [tile_of(f"d{i}") for i in range(2)]
+        square = [tile_of(f"sq{i}") for i in range(2)]
+        damp = [tile_of(f"r{i}") for i in range(2)]
+        pull = [tile_of(f"t{i}") for i in range(2)]
+        part = tile_of("u")
+        res = tile_of("res", align_bytes=DMA_ALIGN)
 
-        centre = by_halves("hc")
-        first_late = keep.tile([P, HALF], F32, name="nb01")
-        second = by_halves("nb1")
-        diff = [by_halves(f"d{i}") for i in range(2)]
-        square = [by_halves(f"sq{i}") for i in range(2)]
-        damp = [by_halves(f"r{i}") for i in range(2)]
-        pull = [by_halves(f"t{i}") for i in range(2)]
-        part = by_halves("u")
-        res = by_halves("res", align_bytes=DMA_ALIGN)
+        def cut(tile, span):
+            return tile[:, span[0] : span[1]]
 
         def look_up(list_tile, span):
             return h[:].indirect(entries(list_tile, span))
+
+        def fused_diff(i, span):
+            nc.vector.tensor_tensor(cut(diff[i], span), look_up(pos_sb[i], span), cut(centre, span), ALU.subtract)
+
+        def plain_diff(i, span):
+            nc.vector.tensor_tensor(cut(diff[i], span), cut(fetched[i], span), cut(centre, span), ALU.subtract)
+
+        def scalar_square(i, span):
+            nc.scalar.activation(cut(square[i], span), cut(diff[i], span), ACT.Square)
+
+        def vector_square(i, span):
+            nc.vector.tensor_tensor(cut(square[i], span), cut(diff[i], span), cut(diff[i], span), ALU.mult)
 
         def root(i, span):
             nc.scalar.activation(cut(damp[i], span), cut(square[i], span), ACT.Abs_reciprocal_sqrt, bias=unit[:])
@@ -152,33 +162,55 @@ def tile_picked_ypm_tv_p_kernel(
         def first_sum(span):
             nc.vector.tensor_tensor(cut(part, span), cut(pull[0], span), cut(centre, span), ALU.add)
 
-        nc.vector.tensor_copy(cut(centre, EARLY), look_up(cen_sb, EARLY))
-        nc.scalar.activation(cut(centre, LATE), look_up(cen_sb, LATE), ACT.Copy)
-        nc.vector.tensor_copy(first_late[:], look_up(pos_sb[0], LATE))
-        for span in (EARLY, LATE):
-            nc.scalar.activation(cut(second, span), look_up(pos_sb[1], span), ACT.Copy)
-        nc.vector.tensor_tensor(cut(diff[0], EARLY), look_up(pos_sb[0], EARLY), cut(centre, EARLY), ALU.subtract)
-        nc.vector.tensor_tensor(cut(diff[0], LATE), first_late[:], cut(centre, LATE), ALU.subtract)
-        for span in (EARLY, LATE):
-            nc.vector.tensor_tensor(cut(diff[1], span), cut(second, span), cut(centre, span), ALU.subtract)
-
-        first_spans = quarters(EARLY) + [LATE]
-        for span in first_spans:
-            nc.scalar.activation(cut(square[0], span), cut(diff[0], span), ACT.Square)
-        for span in first_spans:
-            root(0, span)
-        for span in (EARLY, LATE):
-            nc.vector.tensor_tensor(cut(square[1], span), cut(diff[1], span), cut(diff[1], span), ALU.mult)
-        for span in (EARLY, LATE):
-            root(1, span)
-
-        for span in first_spans:
-            product(0, span)
-        first_sum(EARLY)
-        product(1, EARLY)
-        first_sum(LATE)
-        for span in quarters(LATE):
-            product(1, span)
-        for span, queue in zip([EARLY] + quarters(LATE), (nc.sync, nc.scalar, nc.sync)):
+        def last_sum(span, queue):
             nc.vector.tensor_tensor(cut(res, span), cut(part, span), cut(pull[1], span), ALU.add)
             queue.dma_start(out=out[:, span[0] : span[1]], in_=cut(res, span))
+
+        def vector_fetch(tile, list_tile, span):
+            nc.vector.tensor_copy(cut(tile, span), look_up(list_tile, span))
+
+        def scalar_fetch(tile, list_tile, span):
+            nc.scalar.activation(cut(tile, span), look_up(list_tile, span), ACT.Copy)
+
+        A, B = quarters(EARLY)
+        C, D = quarters(LATE)
+
+        vector_fetch(centre, cen_sb, A)
+        vector_fetch(centre, cen_sb, B)
+        scalar_fetch(centre, cen_sb, LATE)
+        vector_fetch(fetched[0], pos_sb[0], D)
+        scalar_fetch(fetched[1], pos_sb[1], EARLY)
+        scalar_fetch(fetched[1], pos_sb[1], LATE)
+        fused_diff(0, A)
+        fused_diff(0, B)
+        fused_diff(0, C)
+        plain_diff(0, D)
+        plain_diff(1, EARLY)
+        plain_diff(1, LATE)
+        scalar_square(0, A)
+        scalar_square(0, B)
+        scalar_square(0, C)
+        root(0, A)
+        scalar_square(0, D)
+        root(0, B)
+        root(0, C)
+        root(0, D)
+        vector_square(1, EARLY)
+        vector_square(1, C)
+        product(0, A)
+        vector_square(1, D)
+        root(1, EARLY)
+        root(1, C)
+        root(1, D)
+        product(0, B)
+        product(0, C)
+        first_sum(A)
+        product(0, D)
+        first_sum(B)
+        product(1, EARLY)
+        first_sum(LATE)
+        product(1, C)
+        product(1, D)
+        last_sum(EARLY, nc.sync)
+        last_sum(C, nc.scalar)
+        last_sum(D, nc.sync)

@@ -175,16 +175,17 @@ def tile_picked_ypm_tv_p_kernel(
         A, B = quarters(EARLY)
         C, D = quarters(LATE)
 
+        MIDDLE = (B[0], C[1])
         vector_fetch(centre, cen_sb, A)
         vector_fetch(centre, cen_sb, B)
         scalar_fetch(centre, cen_sb, LATE)
-        vector_fetch(fetched[0], pos_sb[0], D)
+        vector_fetch(fetched[0], pos_sb[0], C)
         scalar_fetch(fetched[1], pos_sb[1], EARLY)
         scalar_fetch(fetched[1], pos_sb[1], LATE)
         fused_diff(0, A)
         fused_diff(0, B)
-        fused_diff(0, C)
-        plain_diff(0, D)
+        plain_diff(0, C)
+        fused_diff(0, D)
         plain_diff(1, EARLY)
         plain_diff(1, LATE)
         scalar_square(0, A)
@@ -194,23 +195,23 @@ def tile_picked_ypm_tv_p_kernel(
         scalar_square(0, D)
         root(0, B)
         root(0, C)
+        scalar_square(1, D)
         root(0, D)
         vector_square(1, EARLY)
         vector_square(1, C)
         product(0, A)
-        vector_square(1, D)
-        root(1, EARLY)
-        root(1, C)
+        root(1, A)
+        root(1, MIDDLE)
         root(1, D)
         product(0, B)
         product(0, C)
         first_sum(A)
         product(0, D)
-        first_sum(B)
-        product(1, EARLY)
-        first_sum(LATE)
-        product(1, C)
+        product(1, A)
+        first_sum(MIDDLE)
+        product(1, MIDDLE)
         product(1, D)
-        last_sum(EARLY, nc.sync)
-        last_sum(C, nc.scalar)
+        first_sum(D)
+        last_sum(A, nc.sync)
+        last_sum(MIDDLE, nc.scalar)
         last_sum(D, nc.sync)

@@ -71,18 +71,19 @@ def tile_picked_ypm_tv_p_kernel(
                 out=word_table[g][:].bitcast(I32),
                 in_=x_words[g].rearrange("p n t -> p (n t)").bitcast(I32),
             )
-        nc.sync.dma_start(cen_sb[:], cen)
-        nc.sync.dma_start(pos_sb[0][:], pos1)
-        nc.sync.dma_start(pos_sb[1][:], pos2)
 
         picked_scale = keep.tile([P, S], U8, name="picked_sc", align_bytes=DMA_ALIGN)
         nc.vector.tensor_copy(picked_scale[:], scale_table[:].indirect(offs_sb[:]))
         for j in range(PACK):
             first = ROW0 + ROW_STEP * 2 * j
-            nc.scalar.dma_start(
+            nc.sync.dma_start(
                 out=x_scale[j:P:PACK, :].bitcast(I32),
                 in_=picked_scale[first : first + ROW_STEP * (SCALE_ROWS - 1) + 1 : ROW_STEP, :].bitcast(I32),
             )
+
+        nc.sync.dma_start(cen_sb[:], cen)
+        nc.sync.dma_start(pos_sb[0][:], pos1)
+        nc.sync.dma_start(pos_sb[1][:], pos2)
 
         nc.scalar.activation(unit[:], ones[:], ACT.Abs_reciprocal_sqrt)
 

from contextlib import ExitStack

import concourse.mybir as mybir

K, T, S, V, N = 1024, 2048, 512, 256, 128
FLOPS = 2 * K * N * S

F32 = mybir.dt.float32
BF16 = mybir.dt.bfloat16
I32 = mybir.dt.int32
U32 = mybir.dt.uint32
U16 = mybir.dt.uint16
U8 = mybir.dt.uint8
FP8X4 = mybir.dt.float8_e4m3fn_x4
ACT = mybir.ActivationFunctionType
ALU = mybir.AluOpType

P = 128
PACK = 4
PASSES = K // (P * PACK)
LANES = 16
DMA_ALIGN = 256
MX_ALIGN = 64

ROW0, ROW_STEP = 16, 3
SCALE_ROWS = K // 32

BANKS = [(0, S // 2), (S // 2, 3 * S // 4), (3 * S // 4, S)]

HALF, QUARTER = V // 2, V // 4
EARLY, LATE = (0, HALF), (HALF, V)


def entries(list_tile, span):
    return list_tile[:, span[0] // LANES : span[1] // LANES]


def quarters(span):
    return [(lo, lo + QUARTER) for lo in range(span[0], span[1], QUARTER)]


def tile_picked_ypm_tv_p_kernel(
    tc, x_words, x_scales, w1, rate, offs, cen, pos1, pos2, out
):
    nc = tc.nc
    with ExitStack() as ctx:
        keep = ctx.enter_context(tc.tile_pool(name="keep", bufs=1))
        psum = ctx.enter_context(tc.psum_pool(name="psum", bufs=1))

        offs_sb = keep.tile([P, S // LANES], U16, name="offs_sb")
        cen_sb = keep.tile([P, V // LANES], U16, name="cen_sb")
        pos_sb = [keep.tile([P, V // LANES], U16, name=f"pos_sb{i}") for i in range(2)]
        scale_table = keep.tile([P, T], U8, name="scale_table", align_bytes=DMA_ALIGN)
        word_table = [keep.tile([P, T], U32, name=f"word_table{g}", align_bytes=DMA_ALIGN) for g in range(PASSES)]
        w_raw = keep.tile([P, PASSES, PACK, N], F32, name="w_raw", tag="w_raw", align_bytes=DMA_ALIGN)
        ones = keep.tile([P, 1], F32, name="ones")
        unit = keep.tile([P, 1], F32, name="unit")

        nc.vector.memset(scale_table[:].bitcast(I32), 0)
        nc.vector.memset(ones[:], 1.0)
        x_scale = keep.tile([P, S], U8, name="x_sc", align_bytes=DMA_ALIGN)

        nc.sync.dma_start(out=w_raw[:], in_=w1.rearrange("(g p j) m -> p g j m", g=PASSES, j=PACK))
        nc.sync.dma_start(
            out=scale_table[ROW0 : ROW0 + ROW_STEP * SCALE_ROWS : ROW_STEP].bitcast(I32),
            in_=x_scales.rearrange("g b t -> b g t").bitcast(I32),
        )
        nc.sync.dma_start(offs_sb[:], offs)
        for g in range(PASSES):
            nc.sync.dma_start(
                out=word_table[g][:].bitcast(I32),
                in_=x_words[g].rearrange("p n t -> p (n t)").bitcast(I32),
            )

        picked_scale = keep.tile([P, S], U8, name="picked_sc", align_bytes=DMA_ALIGN)
        nc.vector.tensor_copy(picked_scale[:], scale_table[:].indirect(offs_sb[:]))
        for j in range(PACK):
            first = ROW0 + ROW_STEP * 2 * j
            nc.sync.dma_start(
                out=x_scale[j:P:PACK, :].bitcast(I32),
                in_=picked_scale[first : first + ROW_STEP * (SCALE_ROWS - 1) + 1 : ROW_STEP, :].bitcast(I32),
            )

        nc.sync.dma_start(cen_sb[:], cen)
        nc.sync.dma_start(pos_sb[0][:], pos1)
        nc.sync.dma_start(pos_sb[1][:], pos2)

        nc.scalar.activation(unit[:], ones[:], ACT.Abs_reciprocal_sqrt)

        w_bf = keep.tile([P, PASSES, N, PACK], BF16, name="w_bf", align_bytes=MX_ALIGN)
        for g in range(PASSES):
            nc.scalar.copy(out=w_bf[:, g], in_=w_raw[:, g].rearrange("p j m -> p m j"))

        rate_sb = keep.tile([P, 1], F32, name="rate_sb", tag="w_raw", align_bytes=DMA_ALIGN)
        nc.scalar.dma_start(out=rate_sb[:], in_=rate)

        w_codes = keep.tile([P, PASSES * N], U32, name="w_codes", align_bytes=MX_ALIGN)
        w_scale = keep.tile([P, PASSES * N], U8, name="w_scales", align_bytes=MX_ALIGN)
        nc.vector.quantize_mx(
            out=w_codes[:].bitcast(FP8X4),
            scales=w_scale[:],
            in_=w_bf[:].rearrange("p g m j -> p (g m j)"),
        )

        h = keep.tile([P, S], F32, name="h", align_bytes=MX_ALIGN)
        acc = [psum.tile([P, hi - lo], F32, name=f"acc{lo}") for lo, hi in BANKS]
        gather_spans = [[(0, S // 2), (S // 2, S)], BANKS]
        for g in range(PASSES):
            x_codes = keep.tile([P, S], U32, name=f"x_codes{g}", align_bytes=MX_ALIGN)
            for lo, hi in gather_spans[g]:
                nc.vector.tensor_copy(x_codes[:, lo:hi], word_table[g][:].indirect(entries(offs_sb, (lo, hi))))
            for bank, (lo, hi) in zip(acc, BANKS):
                nc.tensor.matmul_mx(
                    out=bank[:],
                    lhsT=w_codes[:, g * N : (g + 1) * N].bitcast(FP8X4),
                    lhsT_scale=w_scale[:, g * N : (g + 1) * N],
                    rhs=x_codes[:, lo:hi].bitcast(FP8X4),
                    rhs_scale=x_scale[PACK * g :, lo:hi],
                    start=(g == 0),
                    stop=(g == PASSES - 1),
                )
        for bank, (lo, hi) in zip(acc, BANKS):
            nc.scalar.copy(out=h[:, lo:hi], in_=bank[:])

        def tile_of(name, **options):
            return keep.tile([P, V], F32, name=name, **options)

        centre = tile_of("hc")
        fetched = [tile_of(f"nb{i}") for i in range(2)]
        diff = [tile_of(f"d{i}") for i in range(2)]
        square = [tile_of(f"sq{i}") for i in range(2)]
        damp = [tile_of(f"r{i}") for i in range(2)]
        pull = [tile_of(f"t{i}") for i in range(2)]
        part = tile_of("u")
        res = tile_of("res", align_bytes=DMA_ALIGN)

        def cut(tile, span):
            return tile[:, span[0] : span[1]]

        def look_up(list_tile, span):
            return h[:].indirect(entries(list_tile, span))

        def fused_diff(i, span):
            nc.vector.tensor_tensor(cut(diff[i], span), look_up(pos_sb[i], span), cut(centre, span), ALU.subtract)

        def plain_diff(i, span):
            nc.vector.tensor_tensor(cut(diff[i], span), cut(fetched[i], span), cut(centre, span), ALU.subtract)

        def scalar_square(i, span):
            nc.scalar.activation(cut(square[i], span), cut(diff[i], span), ACT.Square)

        def vector_square(i, span):
            nc.vector.tensor_tensor(cut(square[i], span), cut(diff[i], span), cut(diff[i], span), ALU.mult)

        def root(i, span):
            nc.scalar.activation(cut(damp[i], span), cut(square[i], span), ACT.Abs_reciprocal_sqrt, bias=unit[:])

        def product(i, span):
            nc.vector.scalar_tensor_tensor(
                cut(pull[i], span), cut(diff[i], span), rate_sb[:], cut(damp[i], span), ALU.mult, ALU.mult
            )

        def first_sum(span):
            nc.vector.tensor_tensor(cut(part, span), cut(pull[0], span), cut(centre, span), ALU.add)

        def last_sum(span, queue):
            nc.vector.tensor_tensor(cut(res, span), cut(part, span), cut(pull[1], span), ALU.add)
            queue.dma_start(out=out[:, span[0] : span[1]], in_=cut(res, span))

        def vector_fetch(tile, list_tile, span):
            nc.vector.tensor_copy(cut(tile, span), look_up(list_tile, span))

        def scalar_fetch(tile, list_tile, span):
            nc.scalar.activation(cut(tile, span), look_up(list_tile, span), ACT.Copy)

        A, B = quarters(EARLY)
        C, D = quarters(LATE)

        MIDDLE = (B[0], C[1])
        vector_fetch(centre, cen_sb, A)
        vector_fetch(centre, cen_sb, B)
        scalar_fetch(centre, cen_sb, LATE)
        vector_fetch(fetched[0], pos_sb[0], C)
        scalar_fetch(fetched[1], pos_sb[1], EARLY)
        scalar_fetch(fetched[1], pos_sb[1], LATE)
        fused_diff(0, A)
        fused_diff(0, B)
        plain_diff(0, C)
        fused_diff(0, D)
        plain_diff(1, EARLY)
        plain_diff(1, LATE)
        scalar_square(0, A)
        scalar_square(0, B)
        scalar_square(0, C)
        root(0, A)
        scalar_square(0, D)
        root(0, B)
        root(0, C)
        scalar_square(1, D)
        root(0, D)
        vector_square(1, EARLY)
        vector_square(1, C)
        product(0, A)
        root(1, A)
        root(1, MIDDLE)
        root(1, D)
        product(0, B)
        product(0, C)
        first_sum(A)
        product(0, D)
        product(1, A)
        first_sum(MIDDLE)
        product(1, MIDDLE)
        product(1, D)
        first_sum(D)
        last_sum(A, nc.sync)
        last_sum(MIDDLE, nc.scalar)
        last_sum(D, nc.sync)
